import numpy as np
import ml_dtypes


def mxq(x, axis, fmt="e4m3"):
    dtype, down = {"e4m3": (ml_dtypes.float8_e4m3fn, 7), "e5m2": (ml_dtypes.float8_e5m2, 14)}[fmt]
    v = np.moveaxis(np.asarray(x, np.float32).astype(ml_dtypes.bfloat16).astype(np.float64), axis, -1)
    blocks = v.reshape(v.shape[:-1] + (-1, 32))
    amax = np.abs(blocks).max(-1, keepdims=True)
    byte = np.maximum(np.where(amax > 0, np.frexp(amax)[1] - 1 + 127, 0) - down, 1)
    scale = np.exp2(byte - 127.0)
    codes = (blocks / scale).astype(np.float32).astype(dtype).astype(np.float64)
    return np.moveaxis((codes * scale).reshape(v.shape), -1, axis)


WIDE = False


def mx_kscale(k):
    if not WIDE:
        return np.ones(k)
    levels = np.array([10, -10, 5, -5, 0])
    if k % 512:
        return np.exp2(np.random.permutation(np.resize(levels, k // 32))).repeat(32)
    a = np.empty((k // 512, 16))
    for p in range(k // 512):
        a[p, :8] = np.random.permutation(np.resize(levels, 8))
        for g in range(8):
            far = levels[np.abs(levels - a[p, g]) >= 10]
            a[p, g + 8] = far[np.random.randint(len(far))]
    return np.exp2(a.ravel()).repeat(32)


def f64(x):
    return np.asarray(x).astype(np.float64)


def striped(idx):
    return np.tile(idx.reshape(-1, 16).T, (8, 1)).astype(np.uint16)


def unstriped(offs):
    return offs[:16].T.reshape(-1).astype(np.int64)


def pack_weight(w):
    k, n = w.shape
    w = f64(np.asarray(w, np.float32).astype(ml_dtypes.bfloat16)).reshape(k // 32, 32, n)
    amax = np.abs(w).max(1)
    byte = np.clip(np.where(amax > 0, np.frexp(amax)[1] - 1 + 127 - 7, 1), 1, 254)
    scaled = (w * np.exp2(127.0 - byte)[:, None, :]).reshape(k, n).astype(np.float32)
    words = np.ascontiguousarray(scaled.reshape(k // 512, 128, 4, n).transpose(0, 1, 3, 2)).astype(ml_dtypes.float8_e4m3fn).view(np.uint8)
    return words, np.ascontiguousarray(byte.astype(np.uint8).reshape(k // 512, 16, n))


def unpack_weight(words, scales):
    g, p, n, _ = words.shape
    vals = np.ascontiguousarray(words).view(ml_dtypes.float8_e4m3fn).astype(np.float64) * np.repeat(np.exp2(scales.astype(np.float64) - 127.0), 8, axis=1)[..., None]
    return vals.transpose(0, 1, 3, 2).reshape(g * 512, n)


def planes(y):
    n, m = y.shape
    v = y.astype(np.float32).astype(ml_dtypes.bfloat16).astype(np.float64).reshape(n // 32, 32, m)
    top = np.abs(v).max(1)
    byte = np.clip(np.where(top > 0, np.frexp(top)[1] - 1 + 127 - 7, 1), 1, 254)
    codes = (v * np.exp2(127.0 - byte)[:, None, :]).reshape(n, m).astype(np.float32).astype(ml_dtypes.float8_e4m3fn).view(np.uint8)
    words = codes.reshape(n // 512, 128, 4, m).transpose(0, 1, 3, 2)
    return np.ascontiguousarray(words), np.ascontiguousarray(byte.astype(np.uint8).reshape(n // 512, 16, m))


K, T, S, V, H, N = 512, 1024, 512, 256, 512, 512


def setup_inputs():
    n = np.random.standard_normal
    s = mx_kscale(K)[:, None]
    u = mx_kscale(H)
    near = np.random.permutation(S)
    packed_xT = pack_weight(n((K, T)) * s)
    return {
        "x_words": packed_xT[0],
        "x_scales": packed_xT[1],
        "w1": (n((K, H)) / np.sqrt(K) / s * u).astype(np.float32),
        "w2": (n((H, N)) / np.sqrt(H) / u[:, None]).astype(np.float32),
        "el": (np.random.uniform(0.0, 0.8, (H, 1)) * u[:, None]).astype(np.float32),
        "offs": striped(np.random.permutation(T)[:S]),
        "pos1": striped(near[:V]),
        "pos2": striped(near[V:]),
        "pos3": striped(np.random.permutation(S)[:V]),
    }


def reference(x_words, x_scales, w1, w2, el, offs, pos1, pos2, pos3):
    xq = unpack_weight(x_words, x_scales)[:, unstriped(offs)]
    h = mxq(f64(w1), 0, "e4m3").T @ xq
    g0 = h[:, unstriped(pos1)]
    g1 = h[:, unstriped(pos2)]
    g2 = h[:, unstriped(pos3)]
    up = np.maximum(np.maximum(g0, g1), g2) + f64(el)
    lo = np.minimum(np.minimum(g0, g1), g2)
    z = up - lo
    out_0 = mxq(f64(w2), 0, "e4m3").T @ mxq(z, 0, "e4m3")
    return (out_0,) + planes(out_0)

@@ -1,0 +1,282 @@
+from contextlib import ExitStack
+
+import concourse.mybir as mybir
+
+K, T, S, V, H, N = 512, 1024, 512, 256, 512, 512
+FLOPS = 2 * K * H * S + 2 * H * N * V
+
+F32 = mybir.dt.float32
+BF16 = mybir.dt.bfloat16
+I32 = mybir.dt.int32
+U32 = mybir.dt.uint32
+U16 = mybir.dt.uint16
+U8 = mybir.dt.uint8
+FP8X4 = mybir.dt.float8_e4m3fn_x4
+ALU = mybir.AluOpType
+ACT = mybir.ActivationFunctionType
+
+P = 128
+PACK = 4
+LIST_COL = 16
+CHUNK = 128
+
+
+def tile_picked_ymorph_grad_po_kernel(
+    tc, x_words, x_scales, w1, w2, el, offs, pos1, pos2, pos3, out_0, out_1, out_2
+):
+    nc = tc.nc
+    with ExitStack() as ctx:
+        lists = ctx.enter_context(tc.tile_pool(name="lists", bufs=1))
+        keep = ctx.enter_context(tc.tile_pool(name="keep", bufs=1))
+        psum = ctx.enter_context(tc.psum_pool(name="psum", bufs=1))
+
+        offs_sb = lists.tile([P, S // LIST_COL], U16, name="offs_sb")
+        pos_sb = [lists.tile([P, V // LIST_COL], U16, name="pos_sb%d" % i) for i in range(3)]
+
+        xw = keep.tile([P, T], I32, name="xw", align_bytes=64)
+        xs = keep.tile([P, T], U8, name="xs", align_bytes=64)
+        nc.vector.memset(xs[:].bitcast(I32), 0)
+        nc.sync.dma_start(offs_sb[:], offs)
+        nc.sync.dma_start(out=xw[:], in_=x_words[0].rearrange("p n t -> p (n t)").bitcast(I32))
+        for q in range(4):
+            nc.scalar.dma_start(
+                out=xs[32 * q : 32 * q + 4, :].bitcast(I32),
+                in_=x_scales[0, 4 * q : 4 * q + 4, :].bitcast(I32),
+            )
+
+        def load_weight(w, name, edges):
+            rows = w.rearrange("(p j) c -> p j c", j=PACK)
+            pieces = []
+            for a, b in zip(edges[:-1], edges[1:]):
+                raw = keep.tile([P, PACK, b - a], F32, name="%s_raw%d" % (name, a))
+                nc.sync.dma_start(out=raw[:], in_=rows[:, :, a:b])
+                pieces.append((a, b, raw))
+            return pieces
+
+        def deal(engine_copy, grouped, piece):
+            a, b, raw = piece
+            engine_copy(
+                out=grouped[:, :, a // PACK : b // PACK, :].rearrange("p t m j -> p m j t"),
+                in_=raw[:].rearrange("p j (m t) -> p m j t", t=PACK),
+            )
+
+        w1_pieces = load_weight(w1, "w1", [0, 256, 384, 512])
+        for tile_sb, src in zip(pos_sb, (pos1, pos2, pos3)):
+            nc.sync.dma_start(tile_sb[:], src)
+        el_sb = keep.tile([P, PACK], F32, name="el_sb")
+        nc.sync.dma_start(out=el_sb[:], in_=el.rearrange("(p t) o -> p (t o)", t=PACK))
+        w2_pieces = load_weight(w2, "w2", [0, 256, 512])
+
+        xq_s = keep.tile([P, S], U8, name="xq_s", align_bytes=64)
+        xq_w = keep.tile([P, S], U32, name="xq_w", align_bytes=64)
+        nc.vector.tensor_copy(xq_s[:], xs[:].indirect(offs_sb[:]))
+        nc.vector.tensor_copy(xq_w[:], xw[:].bitcast(U32).indirect(offs_sb[:]))
+
+        w1_bf = keep.tile([P, PACK, P, PACK], BF16, name="w1_bf", align_bytes=64)
+        deal(nc.scalar.copy, w1_bf, w1_pieces[0])
+        deal(nc.vector.tensor_copy, w1_bf, w1_pieces[1])
+        deal(nc.vector.tensor_copy, w1_bf, w1_pieces[2])
+        w1_w = keep.tile([P, H], U32, name="w1_w", tag="w1w", align_bytes=64)
+        w1_s = keep.tile([P, H], U8, name="w1_s", align_bytes=64)
+        h = []
+        banks = []
+        for t in range(PACK):
+            cols = slice(t * P, (t + 1) * P)
+            nc.vector.quantize_mx(
+                out=w1_w[:, cols].bitcast(FP8X4),
+                scales=w1_s[:, cols],
+                in_=w1_bf[:, t].rearrange("p m j -> p (m j)"),
+            )
+            h_t = keep.tile([P, S], F32, name="h%d" % t)
+            if t == 0:
+                parts = [(slice(0, S // 2), nc.scalar.copy), (slice(S // 2, S), nc.vector.tensor_copy)]
+            else:
+                parts = [(slice(0, S), nc.scalar.copy)]
+            for places, copy_out in parts:
+                acc = psum.tile([P, places.stop - places.start], F32, name="h_ps", tag="bank%d" % len(banks))
+                banks.append(acc)
+                nc.tensor.matmul_mx(
+                    out=acc[:],
+                    lhsT=w1_w[:, cols].bitcast(FP8X4),
+                    lhsT_scale=w1_s[:, cols],
+                    rhs=xq_w[:, places].bitcast(FP8X4),
+                    rhs_scale=xq_s[:, places],
+                    start=True,
+                    stop=True,
+                )
+                copy_out(out=h_t[:, places], in_=acc[:])
+            h.append(h_t)
+
+        w2_bf = keep.tile([P, PACK, P, PACK], BF16, name="w2_bf", tag="w1w", align_bytes=64)
+        for piece in w2_pieces:
+            deal(nc.scalar.copy, w2_bf, piece)
+        w2_w = keep.tile([P, N], U32, name="w2_w", align_bytes=64)
+        w2_s = keep.tile([P, N], U8, name="w2_s", align_bytes=64)
+
+        g0 = keep.tile([P, PACK, V], F32, name="g0")
+        y_w = keep.tile([P, V], I32, name="y_w", align_bytes=64)
+        y_s = keep.tile([P, V], U8, name="y_s", align_bytes=64)
+        out_rows = out_0.rearrange("(p t) v -> p t v", t=PACK)
+        out_words = out_1[0].rearrange("p n t -> p (n t)").bitcast(I32)
+
+        def pair_tile(name, tag):
+            return keep.tile([P, 2, CHUNK], F32, name=name, tag=tag, align_bytes=64)
+
+        def first(t):
+            nc.vector.tensor_copy(g0[:, t, :], h[t][:].indirect(pos_sb[0][:]))
+
+        def difference(c, t, which, d):
+            cols = slice(c * CHUNK, (c + 1) * CHUNK)
+            lcols = slice(c * CHUNK // LIST_COL, (c + 1) * CHUNK // LIST_COL)
+            nc.vector.tensor_tensor(d[:, t % 2, :], h[t][:].indirect(pos_sb[which][:, lcols]), g0[:, t, cols], ALU.subtract)
+
+        def extreme(out, pair, d1, d2, op):
+            nc.vector.scalar_tensor_tensor(
+                out=out[:, 2 * pair : 2 * pair + 2, :].rearrange("p t v -> p (t v)"),
+                in0=d1[:].rearrange("p t v -> p (t v)"),
+                scalar=0.0,
+                in1=d2[:].rearrange("p t v -> p (t v)"),
+                op0=op,
+                op1=op,
+            )
+
+        def extreme_one(out, t, d1, d2, op):
+            nc.vector.scalar_tensor_tensor(
+                out=out[:, t, :], in0=d1[:, t % 2, :], scalar=0.0, in1=d2[:, t % 2, :], op0=op, op1=op
+            )
+
+        def raise_one(up, hi, t):
+            nc.scalar.activation(out=up[:, t, :], in_=hi[:, t, :], func=ACT.Identity, bias=el_sb[:, t : t + 1])
+
+        def raise_by_el(up, hi, pair):
+            for t in (2 * pair, 2 * pair + 1):
+                nc.scalar.activation(out=up[:, t, :], in_=hi[:, t, :], func=ACT.Identity, bias=el_sb[:, t : t + 1])
+
+        def gradient(z_bf, up, lo):
+            nc.vector.tensor_tensor(
+                z_bf[:].rearrange("p (c i) t -> p c t i", i=4),
+                up[:].rearrange("p t (c i) -> p c t i", i=4),
+                lo[:].rearrange("p t (c i) -> p c t i", i=4),
+                ALU.subtract,
+            )
+
+        def second(c, z_bf):
+            z_w = keep.tile([P, CHUNK], U32, name="z_w%d" % c, align_bytes=64)
+            z_s = keep.tile([P, CHUNK], U8, name="z_s%d" % c, align_bytes=64)
+            nc.vector.quantize_mx(out=z_w[:].bitcast(FP8X4), scales=z_s[:], in_=z_bf[:].rearrange("p v t -> p (v t)"))
+            acc = psum.tile([P, PACK, CHUNK], F32, name="y_ps%d" % c)
+            for t in range(PACK):
+                cols = slice(t * P, (t + 1) * P)
+                nc.tensor.matmul_mx(
+                    out=acc[:, t, :],
+                    lhsT=w2_w[:, cols].bitcast(FP8X4),
+                    lhsT_scale=w2_s[:, cols],
+                    rhs=z_w[:].bitcast(FP8X4),
+                    rhs_scale=z_s[:],
+                    start=True,
+                    stop=True,
+                )
+            return acc
+
+        def leave(c, acc, y_bf, round_copy):
+            cols = slice(c * CHUNK, (c + 1) * CHUNK)
+            round_copy(out=y_bf[:], in_=acc[:].rearrange("p t v -> p v t"))
+            y = keep.tile([P, PACK, CHUNK], F32, name="y%d" % c)
+            nc.scalar.copy(out=y[:], in_=acc[:])
+            nc.sync.dma_start(out=out_rows[:, :, cols], in_=y[:])
+
+        def planes(c, y_bf):
+            cols = slice(c * CHUNK, (c + 1) * CHUNK)
+            nc.vector.quantize_mx(
+                out=y_w[:, cols].bitcast(FP8X4), scales=y_s[:, cols], in_=y_bf[:].rearrange("p v t -> p (v t)")
+            )
+            nc.sync.dma_start(out=out_words[:, cols], in_=y_w[:, cols])
+
+        def quad(name, tag):
+            return keep.tile([P, PACK, CHUNK], F32, name=name, tag=tag, align_bytes=64)
+
+        def rounded(name, tag):
+            return keep.tile([P, CHUNK, PACK], BF16, name=name, tag=tag, align_bytes=64)
+
+        d1a, d2a, d1b, d2b = [pair_tile(n, n) for n in ("d1a", "d2a", "d1b", "d2b")]
+        hi, up, lo = quad("hi0", "hi0"), quad("up0", "up0"), quad("lo0", "lo0")
+        first(0)
+        first(1)
+        difference(0, 0, 1, d1a)
+        difference(0, 0, 2, d2a)
+        first(2)
+        difference(0, 1, 1, d1a)
+        difference(0, 1, 2, d2a)
+        first(3)
+        difference(0, 2, 1, d1b)
+        difference(0, 2, 2, d2b)
+        extreme(hi, 0, d1a, d2a, ALU.max)
+        raise_by_el(up, hi, 0)
+        difference(0, 3, 1, d1b)
+        difference(0, 3, 2, d2b)
+        extreme(lo, 0, d1a, d2a, ALU.min)
+        extreme(hi, 1, d1b, d2b, ALU.max)
+        raise_by_el(up, hi, 1)
+        extreme(lo, 1, d1b, d2b, ALU.min)
+        nc.vector.quantize_mx(
+            out=w2_w[:].bitcast(FP8X4), scales=w2_s[:], in_=w2_bf[:].rearrange("p t m j -> p (t m j)")
+        )
+        z0 = rounded("z0", "z0")
+        e2a = pair_tile("e2a", "e2a")
+        difference(1, 0, 2, e2a)
+        gradient(z0, up, lo)
+        difference(1, 1, 2, e2a)
+        acc0 = second(0, z0)
+        y0 = rounded("ybf0", "ybf0")
+        leave(0, acc0, y0, nc.scalar.copy)
+        e1a = pair_tile("e1a", "up0")
+        e2b = pair_tile("e2b", "z0")
+        difference(1, 0, 1, e1a)
+        difference(1, 1, 1, e1a)
+        difference(1, 2, 2, e2b)
+        difference(1, 3, 2, e2b)
+        hi, up, lo = quad("hi1", "hi1"), quad("up1", "up1"), quad("lo1", "lo1")
+        planes(0, y0)
+        extreme(hi, 0, e1a, e2a, ALU.max)
+        raise_by_el(up, hi, 0)
+        e1b = pair_tile("e1b", "ybf0")
+        difference(1, 2, 1, e1b)
+        extreme(lo, 0, e1a, e2a, ALU.min)
+        extreme_one(hi, 2, e1b, e2b, ALU.max)
+        raise_one(up, hi, 2)
+        difference(1, 3, 1, e1b)
+        extreme_one(lo, 2, e1b, e2b, ALU.min)
+        extreme_one(hi, 3, e1b, e2b, ALU.max)
+        raise_one(up, hi, 3)
+        extreme_one(lo, 3, e1b, e2b, ALU.min)
+        z1 = rounded("z1", "z1")
+        gradient(z1, up, lo)
+        z_w = keep.tile([P, CHUNK], U32, name="z_w1", align_bytes=64)
+        z_s = keep.tile([P, CHUNK], U8, name="z_s1", align_bytes=64)
+        nc.vector.quantize_mx(out=z_w[:].bitcast(FP8X4), scales=z_s[:], in_=z1[:].rearrange("p v t -> p (v t)"))
+        y = keep.tile([P, PACK, CHUNK], F32, name="y1")
+        for t in range(PACK):
+            cols = slice(t * P, (t + 1) * P)
+            acc = psum.tile([P, CHUNK], F32, name="y_ps", tag="bank%d" % t)
+            nc.tensor.matmul_mx(
+                out=acc[:],
+                lhsT=w2_w[:, cols].bitcast(FP8X4),
+                lhsT_scale=w2_s[:, cols],
+                rhs=z_w[:].bitcast(FP8X4),
+                rhs_scale=z_s[:],
+                start=True,
+                stop=True,
+            )
+            nc.scalar.copy(out=y[:, t, :], in_=acc[:])
+        nc.sync.dma_start(out=out_rows[:, :, CHUNK:], in_=y[:])
+        y1 = rounded("ybf1", "ybf1")
+        nc.vector.tensor_copy(
+            out=y1[:].rearrange("p (c i) t -> p c t i", i=4), in_=y[:].rearrange("p t (c i) -> p c t i", i=4)
+        )
+        planes(1, y1)
+        for q in range(4):
+            queue = nc.sync if q % 2 == 0 else nc.scalar
+            queue.dma_start(
+                out=out_2[0, 4 * q : 4 * q + 4, :].bitcast(I32),
+                in_=y_s[32 * q : 32 * q + 4, :].bitcast(I32),
+            )

@@ -18,7 +18,9 @@ ACT = mybir.ActivationFunctionType
 P = 128
 PACK = 4
 LIST_COL = 16
-CHUNK = 128
+EARLY = 192
+LATE = V - EARLY
+EARLY_PARTS = [(0, 128), (128, 192)]
 
 
 def tile_picked_ymorph_grad_po_kernel(
@@ -38,8 +40,9 @@ def tile_picked_ymorph_grad_po_kernel(
         nc.vector.memset(xs[:].bitcast(I32), 0)
         nc.sync.dma_start(offs_sb[:], offs)
         nc.sync.dma_start(out=xw[:], in_=x_words[0].rearrange("p n t -> p (n t)").bitcast(I32))
+        nc.sync.dma_start(pos_sb[0][:], pos1)
         for q in range(4):
-            nc.scalar.dma_start(
+            nc.sync.dma_start(
                 out=xs[32 * q : 32 * q + 4, :].bitcast(I32),
                 in_=x_scales[0, 4 * q : 4 * q + 4, :].bitcast(I32),
             )
@@ -60,9 +63,9 @@ def tile_picked_ymorph_grad_po_kernel(
                 in_=raw[:].rearrange("p j (m t) -> p m j t", t=PACK),
             )
 
-        w1_pieces = load_weight(w1, "w1", [0, 256, 384, 512])
-        for tile_sb, src in zip(pos_sb, (pos1, pos2, pos3)):
-            nc.sync.dma_start(tile_sb[:], src)
+        w1_pieces = load_weight(w1, "w1", [0, 192, 384, 512])
+        nc.sync.dma_start(pos_sb[1][:], pos2)
+        nc.sync.dma_start(pos_sb[2][:], pos3)
         el_sb = keep.tile([P, PACK], F32, name="el_sb")
         nc.sync.dma_start(out=el_sb[:], in_=el.rearrange("(p t) o -> p (t o)", t=PACK))
         w2_pieces = load_weight(w2, "w2", [0, 256, 512])
@@ -74,7 +77,7 @@ def tile_picked_ymorph_grad_po_kernel(
 
         w1_bf = keep.tile([P, PACK, P, PACK], BF16, name="w1_bf", align_bytes=64)
         deal(nc.scalar.copy, w1_bf, w1_pieces[0])
-        deal(nc.vector.tensor_copy, w1_bf, w1_pieces[1])
+        deal(nc.scalar.copy, w1_bf, w1_pieces[1])
         deal(nc.vector.tensor_copy, w1_bf, w1_pieces[2])
         w1_w = keep.tile([P, H], U32, name="w1_w", tag="w1w", align_bytes=64)
         w1_s = keep.tile([P, H], U8, name="w1_s", align_bytes=64)
@@ -113,153 +116,60 @@ def tile_picked_ymorph_grad_po_kernel(
         w2_w = keep.tile([P, N], U32, name="w2_w", align_bytes=64)
         w2_s = keep.tile([P, N], U8, name="w2_s", align_bytes=64)
 
-        g0 = keep.tile([P, PACK, V], F32, name="g0")
         y_w = keep.tile([P, V], I32, name="y_w", align_bytes=64)
         y_s = keep.tile([P, V], U8, name="y_s", align_bytes=64)
         out_rows = out_0.rearrange("(p t) v -> p t v", t=PACK)
         out_words = out_1[0].rearrange("p n t -> p (n t)").bitcast(I32)
+        early, late = slice(0, EARLY), slice(EARLY, V)
 
-        def pair_tile(name, tag):
-            return keep.tile([P, 2, CHUNK], F32, name=name, tag=tag, align_bytes=64)
+        def entries(which, cols):
+            return pos_sb[which][:, cols.start // LIST_COL : cols.stop // LIST_COL]
 
-        def first(t):
-            nc.vector.tensor_copy(g0[:, t, :], h[t][:].indirect(pos_sb[0][:]))
+        def values(name, rows, cols, tag=None):
+            return keep.tile([P, rows, cols.stop - cols.start], F32, name=name, tag=tag or name, align_bytes=64)
 
-        def difference(c, t, which, d):
-            cols = slice(c * CHUNK, (c + 1) * CHUNK)
-            lcols = slice(c * CHUNK // LIST_COL, (c + 1) * CHUNK // LIST_COL)
-            nc.vector.tensor_tensor(d[:, t % 2, :], h[t][:].indirect(pos_sb[which][:, lcols]), g0[:, t, cols], ALU.subtract)
+        def rounded(name, cols, tag=None):
+            return keep.tile([P, cols.stop - cols.start, PACK], BF16, name=name, tag=tag or name, align_bytes=64)
 
-        def extreme(out, pair, d1, d2, op):
+        def first(g0, t, cols):
+            nc.vector.tensor_copy(g0[:, t, :], h[t][:].indirect(entries(0, cols)))
+
+        def difference(d, g0, t, which, cols):
+            nc.vector.tensor_tensor(d[:, t % 2, :], h[t][:].indirect(entries(which, cols)), g0[:, t, :], ALU.subtract)
+
+        def extreme(out, ts, d1, d2, op):
+            rows = slice(ts.start % 2, ts.start % 2 + ts.stop - ts.start)
             nc.vector.scalar_tensor_tensor(
-                out=out[:, 2 * pair : 2 * pair + 2, :].rearrange("p t v -> p (t v)"),
-                in0=d1[:].rearrange("p t v -> p (t v)"),
+                out=out[:, ts, :].rearrange("p t v -> p (t v)"),
+                in0=d1[:, rows, :].rearrange("p t v -> p (t v)"),
                 scalar=0.0,
-                in1=d2[:].rearrange("p t v -> p (t v)"),
+                in1=d2[:, rows, :].rearrange("p t v -> p (t v)"),
                 op0=op,
                 op1=op,
             )
 
-        def extreme_one(out, t, d1, d2, op):
-            nc.vector.scalar_tensor_tensor(
-                out=out[:, t, :], in0=d1[:, t % 2, :], scalar=0.0, in1=d2[:, t % 2, :], op0=op, op1=op
-            )
-
-        def raise_one(up, hi, t):
-            nc.scalar.activation(out=up[:, t, :], in_=hi[:, t, :], func=ACT.Identity, bias=el_sb[:, t : t + 1])
-
-        def raise_by_el(up, hi, pair):
-            for t in (2 * pair, 2 * pair + 1):
+        def raise_by_el(up, hi, ts):
+            for t in range(ts.start, ts.stop):
                 nc.scalar.activation(out=up[:, t, :], in_=hi[:, t, :], func=ACT.Identity, bias=el_sb[:, t : t + 1])
 
-        def gradient(z_bf, up, lo):
+        def gradient(z_bf, up, lo, cols):
             nc.vector.tensor_tensor(
                 z_bf[:].rearrange("p (c i) t -> p c t i", i=4),
-                up[:].rearrange("p t (c i) -> p c t i", i=4),
-                lo[:].rearrange("p t (c i) -> p c t i", i=4),
+                up[:, :, cols].rearrange("p t (c i) -> p c t i", i=4),
+                lo[:, :, cols].rearrange("p t (c i) -> p c t i", i=4),
                 ALU.subtract,
             )
 
-        def second(c, z_bf):
-            z_w = keep.tile([P, CHUNK], U32, name="z_w%d" % c, align_bytes=64)
-            z_s = keep.tile([P, CHUNK], U8, name="z_s%d" % c, align_bytes=64)
+        def quantise_z(z_bf, cols):
+            z_w = keep.tile([P, cols.stop - cols.start], U32, name="z_w%d" % cols.start, align_bytes=64)
+            z_s = keep.tile([P, cols.stop - cols.start], U8, name="z_s%d" % cols.start, align_bytes=64)
             nc.vector.quantize_mx(out=z_w[:].bitcast(FP8X4), scales=z_s[:], in_=z_bf[:].rearrange("p v t -> p (v t)"))
-            acc = psum.tile([P, PACK, CHUNK], F32, name="y_ps%d" % c)
-            for t in range(PACK):
-                cols = slice(t * P, (t + 1) * P)
-                nc.tensor.matmul_mx(
-                    out=acc[:, t, :],
-                    lhsT=w2_w[:, cols].bitcast(FP8X4),
-                    lhsT_scale=w2_s[:, cols],
-                    rhs=z_w[:].bitcast(FP8X4),
-                    rhs_scale=z_s[:],
-                    start=True,
-                    stop=True,
-                )
-            return acc
+            return z_w, z_s
 
-        def leave(c, acc, y_bf, round_copy):
-            cols = slice(c * CHUNK, (c + 1) * CHUNK)
-            round_copy(out=y_bf[:], in_=acc[:].rearrange("p t v -> p v t"))
-            y = keep.tile([P, PACK, CHUNK], F32, name="y%d" % c)
-            nc.scalar.copy(out=y[:], in_=acc[:])
-            nc.sync.dma_start(out=out_rows[:, :, cols], in_=y[:])
-
-        def planes(c, y_bf):
-            cols = slice(c * CHUNK, (c + 1) * CHUNK)
-            nc.vector.quantize_mx(
-                out=y_w[:, cols].bitcast(FP8X4), scales=y_s[:, cols], in_=y_bf[:].rearrange("p v t -> p (v t)")
-            )
-            nc.sync.dma_start(out=out_words[:, cols], in_=y_w[:, cols])
-
-        def quad(name, tag):
-            return keep.tile([P, PACK, CHUNK], F32, name=name, tag=tag, align_bytes=64)
-
-        def rounded(name, tag):
-            return keep.tile([P, CHUNK, PACK], BF16, name=name, tag=tag, align_bytes=64)
-
-        d1a, d2a, d1b, d2b = [pair_tile(n, n) for n in ("d1a", "d2a", "d1b", "d2b")]
-        hi, up, lo = quad("hi0", "hi0"), quad("up0", "up0"), quad("lo0", "lo0")
-        first(0)
-        first(1)
-        difference(0, 0, 1, d1a)
-        difference(0, 0, 2, d2a)
-        first(2)
-        difference(0, 1, 1, d1a)
-        difference(0, 1, 2, d2a)
-        first(3)
-        difference(0, 2, 1, d1b)
-        difference(0, 2, 2, d2b)
-        extreme(hi, 0, d1a, d2a, ALU.max)
-        raise_by_el(up, hi, 0)
-        difference(0, 3, 1, d1b)
-        difference(0, 3, 2, d2b)
-        extreme(lo, 0, d1a, d2a, ALU.min)
-        extreme(hi, 1, d1b, d2b, ALU.max)
-        raise_by_el(up, hi, 1)
-        extreme(lo, 1, d1b, d2b, ALU.min)
-        nc.vector.quantize_mx(
-            out=w2_w[:].bitcast(FP8X4), scales=w2_s[:], in_=w2_bf[:].rearrange("p t m j -> p (t m j)")
-        )
-        z0 = rounded("z0", "z0")
-        e2a = pair_tile("e2a", "e2a")
-        difference(1, 0, 2, e2a)
-        gradient(z0, up, lo)
-        difference(1, 1, 2, e2a)
-        acc0 = second(0, z0)
-        y0 = rounded("ybf0", "ybf0")
-        leave(0, acc0, y0, nc.scalar.copy)
-        e1a = pair_tile("e1a", "up0")
-        e2b = pair_tile("e2b", "z0")
-        difference(1, 0, 1, e1a)
-        difference(1, 1, 1, e1a)
-        difference(1, 2, 2, e2b)
-        difference(1, 3, 2, e2b)
-        hi, up, lo = quad("hi1", "hi1"), quad("up1", "up1"), quad("lo1", "lo1")
-        planes(0, y0)
-        extreme(hi, 0, e1a, e2a, ALU.max)
-        raise_by_el(up, hi, 0)
-        e1b = pair_tile("e1b", "ybf0")
-        difference(1, 2, 1, e1b)
-        extreme(lo, 0, e1a, e2a, ALU.min)
-        extreme_one(hi, 2, e1b, e2b, ALU.max)
-        raise_one(up, hi, 2)
-        difference(1, 3, 1, e1b)
-        extreme_one(lo, 2, e1b, e2b, ALU.min)
-        extreme_one(hi, 3, e1b, e2b, ALU.max)
-        raise_one(up, hi, 3)
-        extreme_one(lo, 3, e1b, e2b, ALU.min)
-        z1 = rounded("z1", "z1")
-        gradient(z1, up, lo)
-        z_w = keep.tile([P, CHUNK], U32, name="z_w1", align_bytes=64)
-        z_s = keep.tile([P, CHUNK], U8, name="z_s1", align_bytes=64)
-        nc.vector.quantize_mx(out=z_w[:].bitcast(FP8X4), scales=z_s[:], in_=z1[:].rearrange("p v t -> p (v t)"))
-        y = keep.tile([P, PACK, CHUNK], F32, name="y1")
-        for t in range(PACK):
+        def second(acc, t, z_w, z_s):
             cols = slice(t * P, (t + 1) * P)
-            acc = psum.tile([P, CHUNK], F32, name="y_ps", tag="bank%d" % t)
             nc.tensor.matmul_mx(
-                out=acc[:],
+                out=acc,
                 lhsT=w2_w[:, cols].bitcast(FP8X4),
                 lhsT_scale=w2_s[:, cols],
                 rhs=z_w[:].bitcast(FP8X4),
@@ -267,13 +177,89 @@ def tile_picked_ymorph_grad_po_kernel(
                 start=True,
                 stop=True,
             )
-            nc.scalar.copy(out=y[:, t, :], in_=acc[:])
-        nc.sync.dma_start(out=out_rows[:, :, CHUNK:], in_=y[:])
-        y1 = rounded("ybf1", "ybf1")
-        nc.vector.tensor_copy(
-            out=y1[:].rearrange("p (c i) t -> p c t i", i=4), in_=y[:].rearrange("p t (c i) -> p c t i", i=4)
+
+        def round_y(y, cols):
+            y_bf = rounded("y_bf%d" % cols.start, cols)
+            nc.vector.tensor_copy(
+                out=y_bf[:].rearrange("p (c i) t -> p c t i", i=4), in_=y[:].rearrange("p t (c i) -> p c t i", i=4)
+            )
+            return y_bf
+
+        def planes(y_bf, cols):
+            nc.vector.quantize_mx(
+                out=y_w[:, cols].bitcast(FP8X4), scales=y_s[:, cols], in_=y_bf[:].rearrange("p v t -> p (v t)")
+            )
+
+        low, high = slice(0, 2), slice(2, 4)
+        g0e, g0l = values("g0e", PACK, early), values("g0l", PACK, late)
+        d1 = [values("d1e%d" % i, 2, early) for i in range(2)]
+        d2 = [values("d2e%d" % i, 2, early) for i in range(2)]
+        hi, up, lo = values("hi_e", PACK, early), values("up_e", PACK, early), values("lo_e", PACK, early)
+        for t in range(PACK):
+            first(g0e, t, early)
+            first(g0l, t, late)
+            difference(d1[t // 2], g0e, t, 1, early)
+            difference(d2[t // 2], g0e, t, 2, early)
+            if t == 2:
+                extreme(hi, low, d1[0], d2[0], ALU.max)
+                raise_by_el(up, hi, low)
+        extreme(lo, low, d1[0], d2[0], ALU.min)
+        extreme(hi, high, d1[1], d2[1], ALU.max)
+        raise_by_el(up, hi, high)
+        extreme(lo, high, d1[1], d2[1], ALU.min)
+        nc.vector.quantize_mx(
+            out=w2_w[:].bitcast(FP8X4), scales=w2_s[:], in_=w2_bf[:].rearrange("p t m j -> p (t m j)")
         )
-        planes(1, y1)
+        parts = [slice(a, b) for a, b in EARLY_PARTS]
+        z_early = [rounded("z_bf%d" % cols.start, cols) for cols in parts]
+        e2 = [values("e2_0", 2, late)]
+        difference(e2[0], g0l, 0, 2, late)
+        difference(e2[0], g0l, 1, 2, late)
+        for z_bf, cols in zip(z_early, parts):
+            gradient(z_bf, up, lo, cols)
+        y_early = []
+        for i, (z_bf, cols) in enumerate(zip(z_early, parts)):
+            z_w, z_s = quantise_z(z_bf, cols)
+            acc = psum.tile([P, PACK, cols.stop - cols.start], F32, name="y_ps", tag="bank%d" % (5 + i))
+            for t in range(PACK):
+                second(acc[:, t, :], t, z_w, z_s)
+            y = values("y%d" % cols.start, PACK, cols)
+            nc.scalar.copy(out=y[:], in_=acc[:])
+            nc.sync.dma_start(out=out_rows[:, :, cols], in_=y[:])
+            y_early.append(y)
+        e1 = [values("e1_0", 2, late, "up_e"), values("e1_1", 2, late, "lo_e")]
+        e2.append(values("e2_1", 2, late, "z_bf0"))
+        difference(e1[0], g0l, 0, 1, late)
+        difference(e1[0], g0l, 1, 1, late)
+        hi, up, lo = values("hi_l", PACK, late), values("up_l", PACK, late), values("lo_l", PACK, late)
+        difference(e1[1], g0l, 2, 1, late)
+        extreme(hi, low, e1[0], e2[0], ALU.max)
+        raise_by_el(up, hi, low)
+        difference(e2[1], g0l, 2, 2, late)
+        extreme(lo, low, e1[0], e2[0], ALU.min)
+        difference(e1[1], g0l, 3, 1, late)
+        extreme(hi, slice(2, 3), e1[1], e2[1], ALU.max)
+        raise_by_el(up, hi, slice(2, 3))
+        difference(e2[1], g0l, 3, 2, late)
+        extreme(lo, slice(2, 3), e1[1], e2[1], ALU.min)
+        extreme(hi, slice(3, 4), e1[1], e2[1], ALU.max)
+        raise_by_el(up, hi, slice(3, 4))
+        extreme(lo, slice(3, 4), e1[1], e2[1], ALU.min)
+        z_late = rounded("z_late", late)
+        gradient(z_late, up, lo, slice(0, LATE))
+        z_w, z_s = quantise_z(z_late, late)
+        y = values("y_late", PACK, late)
+        for t in range(PACK):
+            acc = psum.tile([P, LATE], F32, name="y_ps", tag="bank%d" % t)
+            second(acc[:], t, z_w, z_s)
+            nc.scalar.copy(out=y[:, t, :], in_=acc[:])
+        nc.sync.dma_start(out=out_rows[:, :, late], in_=y[:])
+        y_bfs = [round_y(y_part, cols) for y_part, cols in zip(y_early, parts)]
+        for y_bf, cols in zip(y_bfs, parts):
+            planes(y_bf, cols)
+        nc.sync.dma_start(out=out_words[:, early], in_=y_w[:, early])
+        planes(round_y(y, late), late)
+        nc.sync.dma_start(out=out_words[:, late], in_=y_w[:, late])
         for q in range(4):
             queue = nc.sync if q % 2 == 0 else nc.scalar
             queue.dma_start(

@@ -17,10 +17,15 @@ ACT = mybir.ActivationFunctionType
 
 P = 128
 PACK = 4
+QUADRANT = 32
 LIST_COL = 16
+RUN = 4
+
 EARLY = 192
 LATE = V - EARLY
 EARLY_PARTS = [(0, 128), (128, 192)]
+W1_EDGES = [0, 192, 384, 512]
+W2_EDGES = [0, 256, 512]
 
 
 def tile_picked_ymorph_grad_po_kernel(
@@ -41,10 +46,10 @@ def tile_picked_ymorph_grad_po_kernel(
         nc.sync.dma_start(offs_sb[:], offs)
         nc.sync.dma_start(out=xw[:], in_=x_words[0].rearrange("p n t -> p (n t)").bitcast(I32))
         nc.sync.dma_start(pos_sb[0][:], pos1)
-        for q in range(4):
+        for q in range(P // QUADRANT):
             nc.sync.dma_start(
-                out=xs[32 * q : 32 * q + 4, :].bitcast(I32),
-                in_=x_scales[0, 4 * q : 4 * q + 4, :].bitcast(I32),
+                out=xs[QUADRANT * q : QUADRANT * q + PACK, :].bitcast(I32),
+                in_=x_scales[0, PACK * q : PACK * q + PACK, :].bitcast(I32),
             )
 
         def load_weight(w, name, edges):
@@ -56,19 +61,19 @@ def tile_picked_ymorph_grad_po_kernel(
                 pieces.append((a, b, raw))
             return pieces
 
-        def deal(engine_copy, grouped, piece):
+        def deal(engine_copy, grouped, piece, ts=slice(0, PACK)):
             a, b, raw = piece
             engine_copy(
-                out=grouped[:, :, a // PACK : b // PACK, :].rearrange("p t m j -> p m j t"),
-                in_=raw[:].rearrange("p j (m t) -> p m j t", t=PACK),
+                out=grouped[:, ts, a // PACK : b // PACK, :].rearrange("p t m j -> p m j t"),
+                in_=raw[:].rearrange("p j (m t) -> p m j t", t=PACK)[:, :, :, ts],
             )
 
-        w1_pieces = load_weight(w1, "w1", [0, 192, 384, 512])
+        w1_pieces = load_weight(w1, "w1", W1_EDGES)
         nc.sync.dma_start(pos_sb[1][:], pos2)
         nc.sync.dma_start(pos_sb[2][:], pos3)
         el_sb = keep.tile([P, PACK], F32, name="el_sb")
         nc.sync.dma_start(out=el_sb[:], in_=el.rearrange("(p t) o -> p (t o)", t=PACK))
-        w2_pieces = load_weight(w2, "w2", [0, 256, 512])
+        w2_pieces = load_weight(w2, "w2", W2_EDGES)
 
         xq_s = keep.tile([P, S], U8, name="xq_s", align_bytes=64)
         xq_w = keep.tile([P, S], U32, name="xq_w", align_bytes=64)
@@ -78,7 +83,7 @@ def tile_picked_ymorph_grad_po_kernel(
         w1_bf = keep.tile([P, PACK, P, PACK], BF16, name="w1_bf", align_bytes=64)
         deal(nc.scalar.copy, w1_bf, w1_pieces[0])
         deal(nc.scalar.copy, w1_bf, w1_pieces[1])
-        deal(nc.vector.tensor_copy, w1_bf, w1_pieces[2])
+        deal(nc.vector.tensor_copy, w1_bf, w1_pieces[2], slice(0, 1))
         w1_w = keep.tile([P, H], U32, name="w1_w", tag="w1w", align_bytes=64)
         w1_s = keep.tile([P, H], U8, name="w1_s", align_bytes=64)
         h = []
@@ -92,10 +97,11 @@ def tile_picked_ymorph_grad_po_kernel(
             )
             h_t = keep.tile([P, S], F32, name="h%d" % t)
             if t == 0:
-                parts = [(slice(0, S // 2), nc.scalar.copy), (slice(S // 2, S), nc.vector.tensor_copy)]
+                deal(nc.vector.tensor_copy, w1_bf, w1_pieces[2], slice(1, PACK))
+                shares = [(slice(0, S // 2), nc.scalar.copy), (slice(S // 2, S), nc.vector.tensor_copy)]
             else:
-                parts = [(slice(0, S), nc.scalar.copy)]
-            for places, copy_out in parts:
+                shares = [(slice(0, S), nc.scalar.copy)]
+            for places, copy_out in shares:
                 acc = psum.tile([P, places.stop - places.start], F32, name="h_ps", tag="bank%d" % len(banks))
                 banks.append(acc)
                 nc.tensor.matmul_mx(
@@ -128,8 +134,8 @@ def tile_picked_ymorph_grad_po_kernel(
         def values(name, rows, cols, tag=None):
             return keep.tile([P, rows, cols.stop - cols.start], F32, name=name, tag=tag or name, align_bytes=64)
 
-        def rounded(name, cols, tag=None):
-            return keep.tile([P, cols.stop - cols.start, PACK], BF16, name=name, tag=tag or name, align_bytes=64)
+        def rounded(name, cols):
+            return keep.tile([P, cols.stop - cols.start, PACK], BF16, name=name, tag=name, align_bytes=64)
 
         def first(g0, t, cols):
             nc.vector.tensor_copy(g0[:, t, :], h[t][:].indirect(entries(0, cols)))
@@ -154,9 +160,9 @@ def tile_picked_ymorph_grad_po_kernel(
 
         def gradient(z_bf, up, lo, cols):
             nc.vector.tensor_tensor(
-                z_bf[:].rearrange("p (c i) t -> p c t i", i=4),
-                up[:, :, cols].rearrange("p t (c i) -> p c t i", i=4),
-                lo[:, :, cols].rearrange("p t (c i) -> p c t i", i=4),
+                z_bf[:].rearrange("p (c i) t -> p c t i", i=RUN),
+                up[:, :, cols].rearrange("p t (c i) -> p c t i", i=RUN),
+                lo[:, :, cols].rearrange("p t (c i) -> p c t i", i=RUN),
                 ALU.subtract,
             )
 
@@ -181,11 +187,11 @@ def tile_picked_ymorph_grad_po_kernel(
         def round_y(y, cols):
             y_bf = rounded("y_bf%d" % cols.start, cols)
             nc.vector.tensor_copy(
-                out=y_bf[:].rearrange("p (c i) t -> p c t i", i=4), in_=y[:].rearrange("p t (c i) -> p c t i", i=4)
+                out=y_bf[:].rearrange("p (c i) t -> p c t i", i=RUN), in_=y[:].rearrange("p t (c i) -> p c t i", i=RUN)
             )
             return y_bf
 
-        def planes(y_bf, cols):
+        def quantise_y(y_bf, cols):
             nc.vector.quantize_mx(
                 out=y_w[:, cols].bitcast(FP8X4), scales=y_s[:, cols], in_=y_bf[:].rearrange("p v t -> p (v t)")
             )
@@ -200,7 +206,7 @@ def tile_picked_ymorph_grad_po_kernel(
             first(g0l, t, late)
             difference(d1[t // 2], g0e, t, 1, early)
             difference(d2[t // 2], g0e, t, 2, early)
-            if t == 2:
+            if t == high.start:
                 extreme(hi, low, d1[0], d2[0], ALU.max)
                 raise_by_el(up, hi, low)
         extreme(lo, low, d1[0], d2[0], ALU.min)
@@ -220,13 +226,14 @@ def tile_picked_ymorph_grad_po_kernel(
         y_early = []
         for i, (z_bf, cols) in enumerate(zip(z_early, parts)):
             z_w, z_s = quantise_z(z_bf, cols)
-            acc = psum.tile([P, PACK, cols.stop - cols.start], F32, name="y_ps", tag="bank%d" % (5 + i))
+            acc = psum.tile([P, PACK, cols.stop - cols.start], F32, name="y_ps", tag="bank%d" % (len(banks) + i))
             for t in range(PACK):
                 second(acc[:, t, :], t, z_w, z_s)
             y = values("y%d" % cols.start, PACK, cols)
             nc.scalar.copy(out=y[:], in_=acc[:])
             nc.sync.dma_start(out=out_rows[:, :, cols], in_=y[:])
             y_early.append(y)
+
         e1 = [values("e1_0", 2, late, "up_e"), values("e1_1", 2, late, "lo_e")]
         e2.append(values("e2_1", 2, late, "z_bf0"))
         difference(e1[0], g0l, 0, 1, late)
@@ -237,14 +244,15 @@ def tile_picked_ymorph_grad_po_kernel(
         raise_by_el(up, hi, low)
         difference(e2[1], g0l, 2, 2, late)
         extreme(lo, low, e1[0], e2[0], ALU.min)
+        tile2, tile3 = slice(2, 3), slice(3, 4)
         difference(e1[1], g0l, 3, 1, late)
-        extreme(hi, slice(2, 3), e1[1], e2[1], ALU.max)
-        raise_by_el(up, hi, slice(2, 3))
+        extreme(hi, tile2, e1[1], e2[1], ALU.max)
+        raise_by_el(up, hi, tile2)
         difference(e2[1], g0l, 3, 2, late)
-        extreme(lo, slice(2, 3), e1[1], e2[1], ALU.min)
-        extreme(hi, slice(3, 4), e1[1], e2[1], ALU.max)
-        raise_by_el(up, hi, slice(3, 4))
-        extreme(lo, slice(3, 4), e1[1], e2[1], ALU.min)
+        extreme(lo, tile2, e1[1], e2[1], ALU.min)
+        extreme(hi, tile3, e1[1], e2[1], ALU.max)
+        raise_by_el(up, hi, tile3)
+        extreme(lo, tile3, e1[1], e2[1], ALU.min)
         z_late = rounded("z_late", late)
         gradient(z_late, up, lo, slice(0, LATE))
         z_w, z_s = quantise_z(z_late, late)
@@ -254,15 +262,16 @@ def tile_picked_ymorph_grad_po_kernel(
             second(acc[:], t, z_w, z_s)
             nc.scalar.copy(out=y[:, t, :], in_=acc[:])
         nc.sync.dma_start(out=out_rows[:, :, late], in_=y[:])
+
         y_bfs = [round_y(y_part, cols) for y_part, cols in zip(y_early, parts)]
         for y_bf, cols in zip(y_bfs, parts):
-            planes(y_bf, cols)
+            quantise_y(y_bf, cols)
         nc.sync.dma_start(out=out_words[:, early], in_=y_w[:, early])
-        planes(round_y(y, late), late)
+        quantise_y(round_y(y, late), late)
         nc.sync.dma_start(out=out_words[:, late], in_=y_w[:, late])
-        for q in range(4):
+        for q in range(P // QUADRANT):
             queue = nc.sync if q % 2 == 0 else nc.scalar
             queue.dma_start(
-                out=out_2[0, 4 * q : 4 * q + 4, :].bitcast(I32),
-                in_=y_s[32 * q : 32 * q + 4, :].bitcast(I32),
+                out=out_2[0, PACK * q : PACK * q + PACK, :].bitcast(I32),
+                in_=y_s[QUADRANT * q : QUADRANT * q + PACK, :].bitcast(I32),
             )

@@ -1,6 +1,7 @@
 from contextlib import ExitStack
 
 import concourse.mybir as mybir
+from concourse.masks import make_identity
 
 K, T, S, V, H, N = 512, 1024, 512, 256, 512, 512
 FLOPS = 2 * K * H * S + 2 * H * N * V
@@ -21,11 +22,10 @@ QUADRANT = 32
 LIST_COL = 16
 RUN = 4
 
-EARLY = 192
+EARLY = 128
 LATE = V - EARLY
-EARLY_PARTS = [(0, 128), (128, 192)]
 W1_EDGES = [0, 192, 384, 512]
-W2_EDGES = [0, 256, 512]
+W2_EDGES = [0, 128, 256, 384, 512]
 
 
 def tile_picked_ymorph_grad_po_kernel(
@@ -75,6 +75,9 @@ def tile_picked_ymorph_grad_po_kernel(
         nc.sync.dma_start(out=el_sb[:], in_=el.rearrange("(p t) o -> p (t o)", t=PACK))
         w2_pieces = load_weight(w2, "w2", W2_EDGES)
 
+        ident = keep.tile([P, P], F32, name="ident")
+        make_identity(nc, ident[:])
+
         xq_s = keep.tile([P, S], U8, name="xq_s", align_bytes=64)
         xq_w = keep.tile([P, S], U32, name="xq_w", align_bytes=64)
         nc.vector.tensor_copy(xq_s[:], xs[:].indirect(offs_sb[:]))
@@ -117,8 +120,6 @@ def tile_picked_ymorph_grad_po_kernel(
             h.append(h_t)
 
         w2_bf = keep.tile([P, PACK, P, PACK], BF16, name="w2_bf", tag="w1w", align_bytes=64)
-        for piece in w2_pieces:
-            deal(nc.scalar.copy, w2_bf, piece)
         w2_w = keep.tile([P, N], U32, name="w2_w", align_bytes=64)
         w2_s = keep.tile([P, N], U8, name="w2_s", align_bytes=64)
 
@@ -141,18 +142,10 @@ def tile_picked_ymorph_grad_po_kernel(
             nc.vector.tensor_copy(g0[:, t, :], h[t][:].indirect(entries(0, cols)))
 
         def difference(d, g0, t, which, cols):
-            nc.vector.tensor_tensor(d[:, t % 2, :], h[t][:].indirect(entries(which, cols)), g0[:, t, :], ALU.subtract)
+            nc.vector.tensor_tensor(d, h[t][:].indirect(entries(which, cols)), g0, ALU.subtract)
 
-        def extreme(out, ts, d1, d2, op):
-            rows = slice(ts.start % 2, ts.start % 2 + ts.stop - ts.start)
-            nc.vector.scalar_tensor_tensor(
-                out=out[:, ts, :].rearrange("p t v -> p (t v)"),
-                in0=d1[:, rows, :].rearrange("p t v -> p (t v)"),
-                scalar=0.0,
-                in1=d2[:, rows, :].rearrange("p t v -> p (t v)"),
-                op0=op,
-                op1=op,
-            )
+        def extreme(out, d1, d2, op):
+            nc.vector.scalar_tensor_tensor(out=out, in0=d1, scalar=0.0, in1=d2, op0=op, op1=op)
 
         def raise_by_el(up, hi, ts):
             for t in range(ts.start, ts.stop):
@@ -196,64 +189,68 @@ def tile_picked_ymorph_grad_po_kernel(
                 out=y_w[:, cols].bitcast(FP8X4), scales=y_s[:, cols], in_=y_bf[:].rearrange("p v t -> p (v t)")
             )
 
-        low, high = slice(0, 2), slice(2, 4)
-        g0e, g0l = values("g0e", PACK, early), values("g0l", PACK, late)
-        d1 = [values("d1e%d" % i, 2, early) for i in range(2)]
-        d2 = [values("d2e%d" % i, 2, early) for i in range(2)]
-        hi, up, lo = values("hi_e", PACK, early), values("up_e", PACK, early), values("lo_e", PACK, early)
+        g0e, g0r, d1r = values("g0e", PACK, early), values("g0r", PACK, late), values("d1r", PACK, late)
+        zt_ps = [psum.tile([P, 2, P], F32, name="zt_ps%d" % u, tag="bank%d" % (5 + u)) for u in range(2)]
+        zt_bf = [keep.tile([P, P, 2], BF16, name="zt_bf%d" % u, tag="zt_bf%d" % u, align_bytes=64) for u in range(2)]
+        zw_ps = psum.tile([P, 2, P], F32, name="zw_ps", tag="bank7")
         for t in range(PACK):
+            u, e = divmod(t, 2)
             first(g0e, t, early)
-            first(g0l, t, late)
-            difference(d1[t // 2], g0e, t, 1, early)
-            difference(d2[t // 2], g0e, t, 2, early)
-            if t == high.start:
-                extreme(hi, low, d1[0], d2[0], ALU.max)
-                raise_by_el(up, hi, low)
-        extreme(lo, low, d1[0], d2[0], ALU.min)
-        extreme(hi, high, d1[1], d2[1], ALU.max)
-        raise_by_el(up, hi, high)
-        extreme(lo, high, d1[1], d2[1], ALU.min)
-        nc.vector.quantize_mx(
-            out=w2_w[:].bitcast(FP8X4), scales=w2_s[:], in_=w2_bf[:].rearrange("p t m j -> p (t m j)")
+            first(g0r, t, late)
+            d = values("d%d" % t, 3, early)
+            difference(d[:, 0, :], g0e[:, t, :], t, 1, early)
+            difference(d[:, 1, :], g0e[:, t, :], t, 2, early)
+            difference(d1r[:, t, :], g0r[:, t, :], t, 1, late)
+            nc.vector.tensor_tensor(d[:, 2, :], d[:, 0, :], d[:, 1, :], ALU.subtract)
+            half = values("half%d" % t, 3, early)
+            for rows in [slice(0, 2), slice(2, 3)] if t == PACK - 1 else [slice(0, 3)]:
+                nc.scalar.activation(out=half[:, rows, :], in_=d[:, rows, :], func=ACT.Abs, scale=0.5)
+            if t == PACK - 1:
+                deal(nc.scalar.copy, w2_bf, w2_pieces[t])
+            terms = [el_sb[:, t : t + 1].to_broadcast([P, P])] + [half[:, i, :] for i in range(3)]
+            for i, term in enumerate(terms):
+                nc.tensor.matmul(
+                    out=zt_ps[u][:, e, :], lhsT=term, rhs=ident[:], start=(i == 0), stop=(i == 3), is_transpose=True
+                )
+            if e == 1:
+                nc.scalar.copy(out=zt_bf[u][:], in_=zt_ps[u][:].rearrange("v e p -> v p e"))
+                nc.tensor.transpose(zw_ps[:, u, :], zt_bf[u][:].rearrange("v p e -> v (p e)").bitcast(F32), ident[:])
+            if t < PACK - 1:
+                deal(nc.scalar.copy, w2_bf, w2_pieces[t])
+        z_early = rounded("z_early", early)
+        nc.scalar.copy(
+            out=z_early[:].rearrange("p v t -> p (v t)").bitcast(F32).rearrange("p (v u) -> p v u", u=2),
+            in_=zw_ps[:].rearrange("p u v -> p v u"),
         )
-        parts = [slice(a, b) for a, b in EARLY_PARTS]
-        z_early = [rounded("z_bf%d" % cols.start, cols) for cols in parts]
-        e2 = [values("e2_0", 2, late)]
-        difference(e2[0], g0l, 0, 2, late)
-        difference(e2[0], g0l, 1, 2, late)
-        for z_bf, cols in zip(z_early, parts):
-            gradient(z_bf, up, lo, cols)
-        y_early = []
-        for i, (z_bf, cols) in enumerate(zip(z_early, parts)):
+
+        def product(z_bf, cols, bank):
             z_w, z_s = quantise_z(z_bf, cols)
-            acc = psum.tile([P, PACK, cols.stop - cols.start], F32, name="y_ps", tag="bank%d" % (len(banks) + i))
+            acc = psum.tile([P, PACK, cols.stop - cols.start], F32, name="y_ps", tag=bank)
             for t in range(PACK):
                 second(acc[:, t, :], t, z_w, z_s)
             y = values("y%d" % cols.start, PACK, cols)
             nc.scalar.copy(out=y[:], in_=acc[:])
             nc.sync.dma_start(out=out_rows[:, :, cols], in_=y[:])
-            y_early.append(y)
+            return y
 
-        e1 = [values("e1_0", 2, late, "up_e"), values("e1_1", 2, late, "lo_e")]
-        e2.append(values("e2_1", 2, late, "z_bf0"))
-        difference(e1[0], g0l, 0, 1, late)
-        difference(e1[0], g0l, 1, 1, late)
-        hi, up, lo = values("hi_l", PACK, late), values("up_l", PACK, late), values("lo_l", PACK, late)
-        difference(e1[1], g0l, 2, 1, late)
-        extreme(hi, low, e1[0], e2[0], ALU.max)
-        raise_by_el(up, hi, low)
-        difference(e2[1], g0l, 2, 2, late)
-        extreme(lo, low, e1[0], e2[0], ALU.min)
-        tile2, tile3 = slice(2, 3), slice(3, 4)
-        difference(e1[1], g0l, 3, 1, late)
-        extreme(hi, tile2, e1[1], e2[1], ALU.max)
-        raise_by_el(up, hi, tile2)
-        difference(e2[1], g0l, 3, 2, late)
-        extreme(lo, tile2, e1[1], e2[1], ALU.min)
-        extreme(hi, tile3, e1[1], e2[1], ALU.max)
-        raise_by_el(up, hi, tile3)
-        extreme(lo, tile3, e1[1], e2[1], ALU.min)
-        z_late = rounded("z_late", late)
+        d2r = values("d2r", PACK, late, "g0e")
+        low, high = slice(0, 2), slice(2, 4)
+        hi, up, lo = values("hi", PACK, late), values("up", PACK, late, "half3"), values("lo", PACK, late)
+        for t in range(PACK):
+            difference(d2r[:, t, :], g0r[:, t, :], t, 2, late)
+            if t == high.start:
+                extreme(hi[:, low, :], d1r[:, low, :], d2r[:, low, :], ALU.max)
+                raise_by_el(up, hi, low)
+        extreme(lo[:, low, :], d1r[:, low, :], d2r[:, low, :], ALU.min)
+        extreme(hi[:, high, :], d1r[:, high, :], d2r[:, high, :], ALU.max)
+        raise_by_el(up, hi, high)
+        extreme(lo[:, high, :], d1r[:, high, :], d2r[:, high, :], ALU.min)
+        nc.vector.quantize_mx(
+            out=w2_w[:].bitcast(FP8X4), scales=w2_s[:], in_=w2_bf[:].rearrange("p t m j -> p (t m j)")
+        )
+        parts = [early]
+        y_early = [product(z_early, early, "bank4")]
+        z_late = keep.tile([P, LATE, PACK], BF16, name="z_late", tag="z_early", align_bytes=64)
         gradient(z_late, up, lo, slice(0, LATE))
         z_w, z_s = quantise_z(z_late, late)
         y = values("y_late", PACK, late)
@@ -266,7 +263,7 @@ def tile_picked_ymorph_grad_po_kernel(
         y_bfs = [round_y(y_part, cols) for y_part, cols in zip(y_early, parts)]
         for y_bf, cols in zip(y_bfs, parts):
             quantise_y(y_bf, cols)
-        nc.sync.dma_start(out=out_words[:, early], in_=y_w[:, early])
+        nc.sync.dma_start(out=out_words[:, 0 : late.start], in_=y_w[:, 0 : late.start])
         quantise_y(round_y(y, late), late)
         nc.sync.dma_start(out=out_words[:, late], in_=y_w[:, late])
         for q in range(P // QUADRANT):

@@ -189,7 +189,7 @@ def tile_picked_ymorph_grad_po_kernel(
                 out=y_w[:, cols].bitcast(FP8X4), scales=y_s[:, cols], in_=y_bf[:].rearrange("p v t -> p (v t)")
             )
 
-        g0e, g0r, d1r = values("g0e", PACK, early), values("g0r", PACK, late), values("d1r", PACK, late)
+        g0e, g0r, d1r_last = values("g0e", PACK, early), values("g0r", PACK, late), values("d1r_last", 1, late)
         zt_ps = [psum.tile([P, 2, P], F32, name="zt_ps%d" % u, tag="bank%d" % (5 + u)) for u in range(2)]
         zt_bf = [keep.tile([P, P, 2], BF16, name="zt_bf%d" % u, tag="zt_bf%d" % u, align_bytes=64) for u in range(2)]
         zw_ps = psum.tile([P, 2, P], F32, name="zw_ps", tag="bank7")
@@ -200,8 +200,11 @@ def tile_picked_ymorph_grad_po_kernel(
             d = values("d%d" % t, 3, early)
             difference(d[:, 0, :], g0e[:, t, :], t, 1, early)
             difference(d[:, 1, :], g0e[:, t, :], t, 2, early)
-            difference(d1r[:, t, :], g0r[:, t, :], t, 1, late)
-            nc.vector.tensor_tensor(d[:, 2, :], d[:, 0, :], d[:, 1, :], ALU.subtract)
+            if t < PACK - 1:
+                nc.gpsimd.tensor_tensor(d[:, 2, :], d[:, 0, :], d[:, 1, :], ALU.subtract)
+            else:
+                difference(d1r_last[:, 0, :], g0r[:, t, :], t, 1, late)
+                nc.vector.tensor_tensor(d[:, 2, :], d[:, 0, :], d[:, 1, :], ALU.subtract)
             half = values("half%d" % t, 3, early)
             for rows in [slice(0, 2), slice(2, 3)] if t == PACK - 1 else [slice(0, 3)]:
                 nc.scalar.activation(out=half[:, rows, :], in_=d[:, rows, :], func=ACT.Abs, scale=0.5)
@@ -233,18 +236,18 @@ def tile_picked_ymorph_grad_po_kernel(
             nc.sync.dma_start(out=out_rows[:, :, cols], in_=y[:])
             return y
 
-        d2r = values("d2r", PACK, late, "g0e")
-        low, high = slice(0, 2), slice(2, 4)
-        hi, up, lo = values("hi", PACK, late), values("up", PACK, late, "half3"), values("lo", PACK, late)
+        dr = values("dr", 2 * PACK - 1, late, "g0e")
+        d2r, d1r = dr[:, 0:PACK, :], dr[:, PACK:, :]
+        most, last = slice(0, PACK - 1), slice(PACK - 1, PACK)
+        hi, up, lo = values("hi", PACK, late), values("up", PACK, late, "zt_bf1"), values("lo", PACK, late)
+        for t in range(PACK - 1):
+            difference(d1r[:, t, :], g0r[:, t, :], t, 1, late)
         for t in range(PACK):
             difference(d2r[:, t, :], g0r[:, t, :], t, 2, late)
-            if t == high.start:
-                extreme(hi[:, low, :], d1r[:, low, :], d2r[:, low, :], ALU.max)
-                raise_by_el(up, hi, low)
-        extreme(lo[:, low, :], d1r[:, low, :], d2r[:, low, :], ALU.min)
-        extreme(hi[:, high, :], d1r[:, high, :], d2r[:, high, :], ALU.max)
-        raise_by_el(up, hi, high)
-        extreme(lo[:, high, :], d1r[:, high, :], d2r[:, high, :], ALU.min)
+        for ts, d1_ts in [(most, d1r), (last, d1r_last[:])]:
+            extreme(hi[:, ts, :], d1_ts, d2r[:, ts, :], ALU.max)
+            raise_by_el(up, hi, ts)
+            extreme(lo[:, ts, :], d1_ts, d2r[:, ts, :], ALU.min)
         nc.vector.quantize_mx(
             out=w2_w[:].bitcast(FP8X4), scales=w2_s[:], in_=w2_bf[:].rearrange("p t m j -> p (t m j)")
         )

@@ -42,10 +42,9 @@ def tile_picked_ymorph_grad_po_kernel(
 
         xw = keep.tile([P, T], I32, name="xw", align_bytes=64)
         xs = keep.tile([P, T], U8, name="xs", align_bytes=64)
-        nc.vector.memset(xs[:].bitcast(I32), 0)
-        nc.sync.dma_start(offs_sb[:], offs)
+        nc.gpsimd.memset(xs[:].bitcast(I32), 0)
         nc.sync.dma_start(out=xw[:], in_=x_words[0].rearrange("p n t -> p (n t)").bitcast(I32))
-        nc.sync.dma_start(pos_sb[0][:], pos1)
+        nc.sync.dma_start(offs_sb[:], offs)
         for q in range(P // QUADRANT):
             nc.sync.dma_start(
                 out=xs[QUADRANT * q : QUADRANT * q + PACK, :].bitcast(I32),
@@ -69,6 +68,7 @@ def tile_picked_ymorph_grad_po_kernel(
             )
 
         w1_pieces = load_weight(w1, "w1", W1_EDGES)
+        nc.sync.dma_start(pos_sb[0][:], pos1)
         nc.sync.dma_start(pos_sb[1][:], pos2)
         nc.sync.dma_start(pos_sb[2][:], pos3)
         el_sb = keep.tile([P, PACK], F32, name="el_sb")
@@ -80,12 +80,13 @@ def tile_picked_ymorph_grad_po_kernel(
 
         xq_s = keep.tile([P, S], U8, name="xq_s", align_bytes=64)
         xq_w = keep.tile([P, S], U32, name="xq_w", align_bytes=64)
-        nc.vector.tensor_copy(xq_s[:], xs[:].indirect(offs_sb[:]))
         nc.vector.tensor_copy(xq_w[:], xw[:].bitcast(U32).indirect(offs_sb[:]))
+        nc.vector.tensor_copy(xq_s[:], xs[:].indirect(offs_sb[:]))
 
         w1_bf = keep.tile([P, PACK, P, PACK], BF16, name="w1_bf", align_bytes=64)
         deal(nc.scalar.copy, w1_bf, w1_pieces[0])
-        deal(nc.scalar.copy, w1_bf, w1_pieces[1])
+        deal(nc.scalar.copy, w1_bf, w1_pieces[1], slice(0, 1))
+        deal(nc.scalar.copy, w1_bf, w1_pieces[1], slice(1, PACK))
         deal(nc.vector.tensor_copy, w1_bf, w1_pieces[2], slice(0, 1))
         w1_w = keep.tile([P, H], U32, name="w1_w", tag="w1w", align_bytes=64)
         w1_s = keep.tile([P, H], U8, name="w1_s", align_bytes=64)
@@ -101,7 +102,11 @@ def tile_picked_ymorph_grad_po_kernel(
             h_t = keep.tile([P, S], F32, name="h%d" % t)
             if t == 0:
                 deal(nc.vector.tensor_copy, w1_bf, w1_pieces[2], slice(1, PACK))
-                shares = [(slice(0, S // 2), nc.scalar.copy), (slice(S // 2, S), nc.vector.tensor_copy)]
+                shares = [
+                    (slice(0, S // 2), nc.scalar.copy),
+                    (slice(S // 2, 3 * S // 4), nc.vector.tensor_copy),
+                    (slice(3 * S // 4, S), nc.scalar.copy),
+                ]
             else:
                 shares = [(slice(0, S), nc.scalar.copy)]
             for places, copy_out in shares:
@@ -153,7 +158,7 @@ def tile_picked_ymorph_grad_po_kernel(
 
         def gradient(z_bf, up, lo, cols):
             nc.vector.tensor_tensor(
-                z_bf[:].rearrange("p (c i) t -> p c t i", i=RUN),
+                z_bf.rearrange("p (c i) t -> p c t i", i=RUN),
                 up[:, :, cols].rearrange("p t (c i) -> p c t i", i=RUN),
                 lo[:, :, cols].rearrange("p t (c i) -> p c t i", i=RUN),
                 ALU.subtract,
@@ -180,7 +185,7 @@ def tile_picked_ymorph_grad_po_kernel(
         def round_y(y, cols):
             y_bf = rounded("y_bf%d" % cols.start, cols)
             nc.vector.tensor_copy(
-                out=y_bf[:].rearrange("p (c i) t -> p c t i", i=RUN), in_=y[:].rearrange("p t (c i) -> p c t i", i=RUN)
+                out=y_bf[:].rearrange("p (c i) t -> p c t i", i=RUN), in_=y.rearrange("p t (c i) -> p c t i", i=RUN)
             )
             return y_bf
 
@@ -254,8 +259,15 @@ def tile_picked_ymorph_grad_po_kernel(
         parts = [early]
         y_early = [product(z_early, early, "bank4")]
         z_late = keep.tile([P, LATE, PACK], BF16, name="z_late", tag="z_early", align_bytes=64)
-        gradient(z_late, up, lo, slice(0, LATE))
-        z_w, z_s = quantise_z(z_late, late)
+        halves = [slice(0, LATE // 2), slice(LATE // 2, LATE)]
+        for cols in halves:
+            gradient(z_late[:, cols, :], up, lo, cols)
+        z_w = keep.tile([P, LATE], U32, name="z_w_late", align_bytes=64)
+        z_s = keep.tile([P, LATE], U8, name="z_s_late", align_bytes=64)
+        for cols in halves:
+            nc.vector.quantize_mx(
+                out=z_w[:, cols].bitcast(FP8X4), scales=z_s[:, cols], in_=z_late[:, cols, :].rearrange("p v t -> p (v t)")
+            )
         y = values("y_late", PACK, late)
         for t in range(PACK):
             acc = psum.tile([P, LATE], F32, name="y_ps", tag="bank%d" % t)
@@ -263,11 +275,14 @@ def tile_picked_ymorph_grad_po_kernel(
             nc.scalar.copy(out=y[:, t, :], in_=acc[:])
         nc.sync.dma_start(out=out_rows[:, :, late], in_=y[:])
 
-        y_bfs = [round_y(y_part, cols) for y_part, cols in zip(y_early, parts)]
+        y_bfs = [round_y(y_part[:], cols) for y_part, cols in zip(y_early, parts)]
         for y_bf, cols in zip(y_bfs, parts):
             quantise_y(y_bf, cols)
         nc.sync.dma_start(out=out_words[:, 0 : late.start], in_=y_w[:, 0 : late.start])
-        quantise_y(round_y(y, late), late)
+        late_halves = [slice(late.start + cols.start, late.start + cols.stop) for cols in halves]
+        y_bfs = [round_y(y[:, :, cols], part) for cols, part in zip(halves, late_halves)]
+        for y_bf, part in zip(y_bfs, late_halves):
+            quantise_y(y_bf, part)
         nc.sync.dma_start(out=out_words[:, late], in_=y_w[:, late])
         for q in range(P // QUADRANT):
             queue = nc.sync if q % 2 == 0 else nc.scalar

@@ -24,8 +24,7 @@ RUN = 4
 
 EARLY = 128
 LATE = V - EARLY
-W1_EDGES = [0, 192, 384, 512]
-W2_EDGES = [0, 128, 256, 384, 512]
+W1_PIECES = [(0, 0, 512), (2, 0, 256), (2, 256, 512)]
 
 
 def tile_picked_ymorph_grad_po_kernel(
@@ -51,29 +50,31 @@ def tile_picked_ymorph_grad_po_kernel(
                 in_=x_scales[0, PACK * q : PACK * q + PACK, :].bitcast(I32),
             )
 
-        def load_weight(w, name, edges):
-            rows = w.rearrange("(p j) c -> p j c", j=PACK)
-            pieces = []
-            for a, b in zip(edges[:-1], edges[1:]):
-                raw = keep.tile([P, PACK, b - a], F32, name="%s_raw%d" % (name, a))
-                nc.sync.dma_start(out=raw[:], in_=rows[:, :, a:b])
-                pieces.append((a, b, raw))
-            return pieces
-
         def deal(engine_copy, grouped, piece, ts=slice(0, PACK)):
-            a, b, raw = piece
+            raw, js, cols = piece
             engine_copy(
-                out=grouped[:, ts, a // PACK : b // PACK, :].rearrange("p t m j -> p m j t"),
-                in_=raw[:].rearrange("p j (m t) -> p m j t", t=PACK)[:, :, :, ts],
+                out=grouped[:, ts, cols.start // PACK : cols.stop // PACK, js].rearrange("p t m j -> p m j t"),
+                in_=raw.rearrange("p j (m t) -> p m j t", t=PACK)[:, :, :, ts],
             )
 
-        w1_pieces = load_weight(w1, "w1", W1_EDGES)
+        w1_rows = w1.rearrange("(p j) c -> p j c", j=PACK)
+        w1_pieces = []
+        for j, a, b in W1_PIECES:
+            raw = keep.tile([P, 2, b - a], F32, name="w1_raw%d_%d" % (j, a))
+            nc.sync.dma_start(out=raw[:], in_=w1_rows[:, j : j + 2, a:b])
+            w1_pieces.append((raw[:], slice(j, j + 2), slice(a, b)))
         nc.sync.dma_start(pos_sb[0][:], pos1)
         nc.sync.dma_start(pos_sb[1][:], pos2)
         nc.sync.dma_start(pos_sb[2][:], pos3)
         el_sb = keep.tile([P, PACK], F32, name="el_sb")
         nc.sync.dma_start(out=el_sb[:], in_=el.rearrange("(p t) o -> p (t o)", t=PACK))
-        w2_pieces = load_weight(w2, "w2", W2_EDGES)
+        w2_rows = w2.rearrange("(p j) c -> p j c", j=PACK)
+        w2_pieces = []
+        for a in range(0, N, 2 * P):
+            raw = keep.tile([P, PACK, 2 * P], F32, name="w2_raw%d" % a)
+            nc.sync.dma_start(out=raw[:], in_=w2_rows[:, :, a : a + 2 * P])
+            for b in (0, P):
+                w2_pieces.append((raw[:, :, b : b + P], slice(0, PACK), slice(a + b, a + b + P)))
 
         ident = keep.tile([P, P], F32, name="ident")
         make_identity(nc, ident[:])
@@ -84,9 +85,9 @@ def tile_picked_ymorph_grad_po_kernel(
         nc.vector.tensor_copy(xq_s[:], xs[:].indirect(offs_sb[:]))
 
         w1_bf = keep.tile([P, PACK, P, PACK], BF16, name="w1_bf", align_bytes=64)
-        deal(nc.scalar.copy, w1_bf, w1_pieces[0])
-        deal(nc.scalar.copy, w1_bf, w1_pieces[1], slice(0, 1))
-        deal(nc.scalar.copy, w1_bf, w1_pieces[1], slice(1, PACK))
+        deal(nc.scalar.copy, w1_bf, w1_pieces[0], slice(0, 2))
+        deal(nc.scalar.copy, w1_bf, w1_pieces[0], slice(2, PACK))
+        deal(nc.vector.tensor_copy, w1_bf, w1_pieces[1])
         deal(nc.vector.tensor_copy, w1_bf, w1_pieces[2], slice(0, 1))
         w1_w = keep.tile([P, H], U32, name="w1_w", tag="w1w", align_bytes=64)
         w1_s = keep.tile([P, H], U8, name="w1_s", align_bytes=64)

@@ -18,13 +18,14 @@ ACT = mybir.ActivationFunctionType
 
 P = 128
 PACK = 4
+PAIR = 2
 QUADRANT = 32
 LIST_COL = 16
 RUN = 4
 
-EARLY = 128
+EARLY = P
 LATE = V - EARLY
-W1_PIECES = [(0, 0, 512), (2, 0, 256), (2, 256, 512)]
+W1_PIECES = [(0, 0, H), (PAIR, 0, H // 2), (PAIR, H // 2, H)]
 
 
 def tile_picked_ymorph_grad_po_kernel(
@@ -50,6 +51,27 @@ def tile_picked_ymorph_grad_po_kernel(
                 in_=x_scales[0, PACK * q : PACK * q + PACK, :].bitcast(I32),
             )
 
+        w1_rows = w1.rearrange("(p j) c -> p j c", j=PACK)
+        w1_pieces = []
+        for j, a, b in W1_PIECES:
+            raw = keep.tile([P, PAIR, b - a], F32, name="w1_raw%d_%d" % (j, a))
+            nc.sync.dma_start(out=raw[:], in_=w1_rows[:, j : j + PAIR, a:b])
+            w1_pieces.append((raw[:], slice(j, j + PAIR), slice(a, b)))
+        for list_sb, pos in zip(pos_sb, [pos1, pos2, pos3]):
+            nc.sync.dma_start(list_sb[:], pos)
+        el_sb = keep.tile([P, PACK], F32, name="el_sb")
+        nc.sync.dma_start(out=el_sb[:], in_=el.rearrange("(p t) o -> p (t o)", t=PACK))
+        w2_rows = w2.rearrange("(p j) c -> p j c", j=PACK)
+        w2_pieces = []
+        for a in range(0, N, N // 2):
+            raw = keep.tile([P, PACK, N // 2], F32, name="w2_raw%d" % a)
+            nc.sync.dma_start(out=raw[:], in_=w2_rows[:, :, a : a + N // 2])
+            for b in range(0, N // 2, N // 4):
+                w2_pieces.append((raw[:, :, b : b + N // 4], slice(0, PACK), slice(a + b, a + b + N // 4)))
+
+        ident = keep.tile([P, P], F32, name="ident")
+        make_identity(nc, ident[:])
+
         def deal(engine_copy, grouped, piece, ts=slice(0, PACK)):
             raw, js, cols = piece
             engine_copy(
@@ -57,27 +79,10 @@ def tile_picked_ymorph_grad_po_kernel(
                 in_=raw.rearrange("p j (m t) -> p m j t", t=PACK)[:, :, :, ts],
             )
 
-        w1_rows = w1.rearrange("(p j) c -> p j c", j=PACK)
-        w1_pieces = []
-        for j, a, b in W1_PIECES:
-            raw = keep.tile([P, 2, b - a], F32, name="w1_raw%d_%d" % (j, a))
-            nc.sync.dma_start(out=raw[:], in_=w1_rows[:, j : j + 2, a:b])
-            w1_pieces.append((raw[:], slice(j, j + 2), slice(a, b)))
-        nc.sync.dma_start(pos_sb[0][:], pos1)
-        nc.sync.dma_start(pos_sb[1][:], pos2)
-        nc.sync.dma_start(pos_sb[2][:], pos3)
-        el_sb = keep.tile([P, PACK], F32, name="el_sb")
-        nc.sync.dma_start(out=el_sb[:], in_=el.rearrange("(p t) o -> p (t o)", t=PACK))
-        w2_rows = w2.rearrange("(p j) c -> p j c", j=PACK)
-        w2_pieces = []
-        for a in range(0, N, 2 * P):
-            raw = keep.tile([P, PACK, 2 * P], F32, name="w2_raw%d" % a)
-            nc.sync.dma_start(out=raw[:], in_=w2_rows[:, :, a : a + 2 * P])
-            for b in (0, P):
-                w2_pieces.append((raw[:, :, b : b + P], slice(0, PACK), slice(a + b, a + b + P)))
+        def bank(number, name, shape):
+            return psum.tile(shape, F32, name=name, tag="bank%d" % number)
 
-        ident = keep.tile([P, P], F32, name="ident")
-        make_identity(nc, ident[:])
+        low, high = slice(0, PAIR), slice(PAIR, PACK)
 
         xq_s = keep.tile([P, S], U8, name="xq_s", align_bytes=64)
         xq_w = keep.tile([P, S], U32, name="xq_w", align_bytes=64)
@@ -85,24 +90,26 @@ def tile_picked_ymorph_grad_po_kernel(
         nc.vector.tensor_copy(xq_s[:], xs[:].indirect(offs_sb[:]))
 
         w1_bf = keep.tile([P, PACK, P, PACK], BF16, name="w1_bf", align_bytes=64)
-        deal(nc.scalar.copy, w1_bf, w1_pieces[0], slice(0, 2))
-        deal(nc.scalar.copy, w1_bf, w1_pieces[0], slice(2, PACK))
+        deal(nc.scalar.copy, w1_bf, w1_pieces[0], low)
+        deal(nc.scalar.copy, w1_bf, w1_pieces[0], high)
         deal(nc.vector.tensor_copy, w1_bf, w1_pieces[1])
         deal(nc.vector.tensor_copy, w1_bf, w1_pieces[2], slice(0, 1))
         w1_w = keep.tile([P, H], U32, name="w1_w", tag="w1w", align_bytes=64)
         w1_s = keep.tile([P, H], U8, name="w1_s", align_bytes=64)
         h = []
-        banks = []
+        banks_used = 0
         for t in range(PACK):
             cols = slice(t * P, (t + 1) * P)
-            nc.vector.quantize_mx(
-                out=w1_w[:, cols].bitcast(FP8X4),
-                scales=w1_s[:, cols],
-                in_=w1_bf[:, t].rearrange("p m j -> p (m j)"),
-            )
+            for ms in [slice(0, P // 2), slice(P // 2, P)] if t == 0 else [slice(0, P)]:
+                nc.vector.quantize_mx(
+                    out=w1_w[:, cols][:, ms].bitcast(FP8X4),
+                    scales=w1_s[:, cols][:, ms],
+                    in_=w1_bf[:, t, ms].rearrange("p m j -> p (m j)"),
+                )
             h_t = keep.tile([P, S], F32, name="h%d" % t)
             if t == 0:
-                deal(nc.vector.tensor_copy, w1_bf, w1_pieces[2], slice(1, PACK))
+                deal(nc.vector.tensor_copy, w1_bf, w1_pieces[2], slice(1, PAIR))
+                deal(nc.scalar.copy, w1_bf, w1_pieces[2], high)
                 shares = [
                     (slice(0, S // 2), nc.scalar.copy),
                     (slice(S // 2, 3 * S // 4), nc.vector.tensor_copy),
@@ -111,8 +118,8 @@ def tile_picked_ymorph_grad_po_kernel(
             else:
                 shares = [(slice(0, S), nc.scalar.copy)]
             for places, copy_out in shares:
-                acc = psum.tile([P, places.stop - places.start], F32, name="h_ps", tag="bank%d" % len(banks))
-                banks.append(acc)
+                acc = bank(banks_used, "h_ps", [P, places.stop - places.start])
+                banks_used = banks_used + 1
                 nc.tensor.matmul_mx(
                     out=acc[:],
                     lhsT=w1_w[:, cols].bitcast(FP8X4),
@@ -134,6 +141,7 @@ def tile_picked_ymorph_grad_po_kernel(
         out_rows = out_0.rearrange("(p t) v -> p t v", t=PACK)
         out_words = out_1[0].rearrange("p n t -> p (n t)").bitcast(I32)
         early, late = slice(0, EARLY), slice(EARLY, V)
+        halves = [slice(0, P // 2), slice(P // 2, P)]
 
         def entries(which, cols):
             return pos_sb[which][:, cols.start // LIST_COL : cols.stop // LIST_COL]
@@ -148,28 +156,13 @@ def tile_picked_ymorph_grad_po_kernel(
             nc.vector.tensor_copy(g0[:, t, :], h[t][:].indirect(entries(0, cols)))
 
         def difference(d, g0, t, which, cols):
-            nc.vector.tensor_tensor(d, h[t][:].indirect(entries(which, cols)), g0, ALU.subtract)
+            nc.vector.tensor_tensor(d, h[t][:].indirect(entries(which, cols)), g0[:, t, :], ALU.subtract)
 
         def extreme(out, d1, d2, op):
             nc.vector.scalar_tensor_tensor(out=out, in0=d1, scalar=0.0, in1=d2, op0=op, op1=op)
 
-        def raise_by_el(up, hi, ts):
-            for t in range(ts.start, ts.stop):
-                nc.scalar.activation(out=up[:, t, :], in_=hi[:, t, :], func=ACT.Identity, bias=el_sb[:, t : t + 1])
-
-        def gradient(z_bf, up, lo, cols):
-            nc.vector.tensor_tensor(
-                z_bf.rearrange("p (c i) t -> p c t i", i=RUN),
-                up[:, :, cols].rearrange("p t (c i) -> p c t i", i=RUN),
-                lo[:, :, cols].rearrange("p t (c i) -> p c t i", i=RUN),
-                ALU.subtract,
-            )
-
-        def quantise_z(z_bf, cols):
-            z_w = keep.tile([P, cols.stop - cols.start], U32, name="z_w%d" % cols.start, align_bytes=64)
-            z_s = keep.tile([P, cols.stop - cols.start], U8, name="z_s%d" % cols.start, align_bytes=64)
-            nc.vector.quantize_mx(out=z_w[:].bitcast(FP8X4), scales=z_s[:], in_=z_bf[:].rearrange("p v t -> p (v t)"))
-            return z_w, z_s
+        def quantise(words, scales, grouped):
+            nc.vector.quantize_mx(out=words.bitcast(FP8X4), scales=scales, in_=grouped.rearrange("p v t -> p (v t)"))
 
         def second(acc, t, z_w, z_s):
             cols = slice(t * P, (t + 1) * P)
@@ -183,48 +176,55 @@ def tile_picked_ymorph_grad_po_kernel(
                 stop=True,
             )
 
-        def round_y(y, cols):
-            y_bf = rounded("y_bf%d" % cols.start, cols)
-            nc.vector.tensor_copy(
-                out=y_bf[:].rearrange("p (c i) t -> p c t i", i=RUN), in_=y.rearrange("p t (c i) -> p c t i", i=RUN)
-            )
-            return y_bf
+        def planes(y, group):
+            parts = [slice(group.start + half.start, group.start + half.stop) for half in halves]
+            y_bfs = [rounded("y_bf%d" % part.start, part) for part in parts]
+            for y_bf, half in zip(y_bfs, halves):
+                nc.vector.tensor_copy(
+                    out=y_bf[:].rearrange("p (c i) t -> p c t i", i=RUN),
+                    in_=y[:, :, half].rearrange("p t (c i) -> p c t i", i=RUN),
+                )
+            for y_bf, part in zip(y_bfs, parts):
+                quantise(y_w[:, part], y_s[:, part], y_bf[:])
+            nc.sync.dma_start(out=out_words[:, group], in_=y_w[:, group])
 
-        def quantise_y(y_bf, cols):
-            nc.vector.quantize_mx(
-                out=y_w[:, cols].bitcast(FP8X4), scales=y_s[:, cols], in_=y_bf[:].rearrange("p v t -> p (v t)")
-            )
-
-        g0e, g0r, d1r_last = values("g0e", PACK, early), values("g0r", PACK, late), values("d1r_last", 1, late)
-        zt_ps = [psum.tile([P, 2, P], F32, name="zt_ps%d" % u, tag="bank%d" % (5 + u)) for u in range(2)]
-        zt_bf = [keep.tile([P, P, 2], BF16, name="zt_bf%d" % u, tag="zt_bf%d" % u, align_bytes=64) for u in range(2)]
-        zw_ps = psum.tile([P, 2, P], F32, name="zw_ps", tag="bank7")
+        g0_early, g0_late = values("g0_early", PACK, early), values("g0_late", PACK, late)
+        d1_last = values("d1_last", 1, late)
+        zt_ps = [bank(5 + u, "zt_ps%d" % u, [P, PAIR, P]) for u in range(2)]
+        zt_bf = [keep.tile([P, P, PAIR], BF16, name="zt_bf%d" % u, tag="zt_bf%d" % u, align_bytes=64) for u in range(2)]
+        zw_ps = bank(7, "zw_ps", [P, 2, P])
         for t in range(PACK):
-            u, e = divmod(t, 2)
-            first(g0e, t, early)
-            first(g0r, t, late)
+            u, e = divmod(t, PAIR)
+            is_last = t == PACK - 1
+            first(g0_early, t, early)
+            first(g0_late, t, late)
             d = values("d%d" % t, 3, early)
-            difference(d[:, 0, :], g0e[:, t, :], t, 1, early)
-            difference(d[:, 1, :], g0e[:, t, :], t, 2, early)
-            if t < PACK - 1:
-                nc.gpsimd.tensor_tensor(d[:, 2, :], d[:, 0, :], d[:, 1, :], ALU.subtract)
-            else:
-                difference(d1r_last[:, 0, :], g0r[:, t, :], t, 1, late)
+            difference(d[:, 0, :], g0_early, t, 1, early)
+            difference(d[:, 1, :], g0_early, t, 2, early)
+            if is_last:
+                difference(d1_last[:, 0, :], g0_late, t, 1, late)
                 nc.vector.tensor_tensor(d[:, 2, :], d[:, 0, :], d[:, 1, :], ALU.subtract)
-            half = values("half%d" % t, 3, early)
-            for rows in [slice(0, 2), slice(2, 3)] if t == PACK - 1 else [slice(0, 3)]:
-                nc.scalar.activation(out=half[:, rows, :], in_=d[:, rows, :], func=ACT.Abs, scale=0.5)
-            if t == PACK - 1:
+            else:
+                nc.gpsimd.tensor_tensor(d[:, 2, :], d[:, 0, :], d[:, 1, :], ALU.subtract)
+            halved = values("halved%d" % t, 3, early)
+            for rows in [slice(0, 2), slice(2, 3)] if is_last else [slice(0, 3)]:
+                nc.scalar.activation(out=halved[:, rows, :], in_=d[:, rows, :], func=ACT.Abs, scale=0.5)
+            if is_last:
                 deal(nc.scalar.copy, w2_bf, w2_pieces[t])
-            terms = [el_sb[:, t : t + 1].to_broadcast([P, P])] + [half[:, i, :] for i in range(3)]
+            terms = [el_sb[:, t : t + 1].to_broadcast([P, P])] + [halved[:, i, :] for i in range(3)]
             for i, term in enumerate(terms):
                 nc.tensor.matmul(
-                    out=zt_ps[u][:, e, :], lhsT=term, rhs=ident[:], start=(i == 0), stop=(i == 3), is_transpose=True
+                    out=zt_ps[u][:, e, :],
+                    lhsT=term,
+                    rhs=ident[:],
+                    start=(i == 0),
+                    stop=(i == len(terms) - 1),
+                    is_transpose=True,
                 )
-            if e == 1:
+            if e == PAIR - 1:
                 nc.scalar.copy(out=zt_bf[u][:], in_=zt_ps[u][:].rearrange("v e p -> v p e"))
                 nc.tensor.transpose(zw_ps[:, u, :], zt_bf[u][:].rearrange("v p e -> v (p e)").bitcast(F32), ident[:])
-            if t < PACK - 1:
+            if not is_last:
                 deal(nc.scalar.copy, w2_bf, w2_pieces[t])
         z_early = rounded("z_early", early)
         nc.scalar.copy(
@@ -232,59 +232,54 @@ def tile_picked_ymorph_grad_po_kernel(
             in_=zw_ps[:].rearrange("p u v -> p v u"),
         )
 
-        def product(z_bf, cols, bank):
-            z_w, z_s = quantise_z(z_bf, cols)
-            acc = psum.tile([P, PACK, cols.stop - cols.start], F32, name="y_ps", tag=bank)
-            for t in range(PACK):
-                second(acc[:, t, :], t, z_w, z_s)
-            y = values("y%d" % cols.start, PACK, cols)
-            nc.scalar.copy(out=y[:], in_=acc[:])
-            nc.sync.dma_start(out=out_rows[:, :, cols], in_=y[:])
-            return y
-
-        dr = values("dr", 2 * PACK - 1, late, "g0e")
-        d2r, d1r = dr[:, 0:PACK, :], dr[:, PACK:, :]
+        d_late = values("d_late", 2 * PACK - 1, late, "g0_early")
+        d2_late, d1_most = d_late[:, 0:PACK, :], d_late[:, PACK:, :]
         most, last = slice(0, PACK - 1), slice(PACK - 1, PACK)
         hi, up, lo = values("hi", PACK, late), values("up", PACK, late, "zt_bf1"), values("lo", PACK, late)
         for t in range(PACK - 1):
-            difference(d1r[:, t, :], g0r[:, t, :], t, 1, late)
+            difference(d1_most[:, t, :], g0_late, t, 1, late)
         for t in range(PACK):
-            difference(d2r[:, t, :], g0r[:, t, :], t, 2, late)
-        for ts, d1_ts in [(most, d1r), (last, d1r_last[:])]:
-            extreme(hi[:, ts, :], d1_ts, d2r[:, ts, :], ALU.max)
-            raise_by_el(up, hi, ts)
-            extreme(lo[:, ts, :], d1_ts, d2r[:, ts, :], ALU.min)
-        nc.vector.quantize_mx(
-            out=w2_w[:].bitcast(FP8X4), scales=w2_s[:], in_=w2_bf[:].rearrange("p t m j -> p (t m j)")
-        )
-        parts = [early]
-        y_early = [product(z_early, early, "bank4")]
-        z_late = keep.tile([P, LATE, PACK], BF16, name="z_late", tag="z_early", align_bytes=64)
-        halves = [slice(0, LATE // 2), slice(LATE // 2, LATE)]
-        for cols in halves:
-            gradient(z_late[:, cols, :], up, lo, cols)
-        z_w = keep.tile([P, LATE], U32, name="z_w_late", align_bytes=64)
-        z_s = keep.tile([P, LATE], U8, name="z_s_late", align_bytes=64)
-        for cols in halves:
-            nc.vector.quantize_mx(
-                out=z_w[:, cols].bitcast(FP8X4), scales=z_s[:, cols], in_=z_late[:, cols, :].rearrange("p v t -> p (v t)")
-            )
-        y = values("y_late", PACK, late)
-        for t in range(PACK):
-            acc = psum.tile([P, LATE], F32, name="y_ps", tag="bank%d" % t)
-            second(acc[:], t, z_w, z_s)
-            nc.scalar.copy(out=y[:, t, :], in_=acc[:])
-        nc.sync.dma_start(out=out_rows[:, :, late], in_=y[:])
+            difference(d2_late[:, t, :], g0_late, t, 2, late)
+        for ts, d1_ts in [(most, d1_most), (last, d1_last[:])]:
+            extreme(hi[:, ts, :], d1_ts, d2_late[:, ts, :], ALU.max)
+            for t in range(ts.start, ts.stop):
+                nc.scalar.activation(out=up[:, t, :], in_=hi[:, t, :], func=ACT.Identity, bias=el_sb[:, t : t + 1])
+            extreme(lo[:, ts, :], d1_ts, d2_late[:, ts, :], ALU.min)
 
-        y_bfs = [round_y(y_part[:], cols) for y_part, cols in zip(y_early, parts)]
-        for y_bf, cols in zip(y_bfs, parts):
-            quantise_y(y_bf, cols)
-        nc.sync.dma_start(out=out_words[:, 0 : late.start], in_=y_w[:, 0 : late.start])
-        late_halves = [slice(late.start + cols.start, late.start + cols.stop) for cols in halves]
-        y_bfs = [round_y(y[:, :, cols], part) for cols, part in zip(halves, late_halves)]
-        for y_bf, part in zip(y_bfs, late_halves):
-            quantise_y(y_bf, part)
-        nc.sync.dma_start(out=out_words[:, late], in_=y_w[:, late])
+        quantise(w2_w[:], w2_s[:], w2_bf[:].rearrange("p t m j -> p (t m) j"))
+        ze_w = keep.tile([P, EARLY], U32, name="ze_w", align_bytes=64)
+        ze_s = keep.tile([P, EARLY], U8, name="ze_s", align_bytes=64)
+        quantise(ze_w[:], ze_s[:], z_early[:])
+        pair_ps = [bank(4 + u, "pair_ps%d" % u, [P, PAIR, EARLY]) for u in range(2)]
+        for t in range(PACK):
+            second(pair_ps[t // PAIR][:, t % PAIR, :], t, ze_w, ze_s)
+
+        z_late = rounded("z_late", late)
+        for half in halves:
+            nc.vector.tensor_tensor(
+                z_late[:, half, :].rearrange("p (c i) t -> p c t i", i=RUN),
+                up[:, :, half].rearrange("p t (c i) -> p c t i", i=RUN),
+                lo[:, :, half].rearrange("p t (c i) -> p c t i", i=RUN),
+                ALU.subtract,
+            )
+        zl_w = keep.tile([P, LATE], U32, name="zl_w", align_bytes=64)
+        zl_s = keep.tile([P, LATE], U8, name="zl_s", align_bytes=64)
+        for half in halves:
+            quantise(zl_w[:, half], zl_s[:, half], z_late[:, half, :])
+
+        y_early = values("y_early", PACK, early, "z_late")
+        nc.scalar.copy(out=y_early[:, low, :], in_=pair_ps[0][:])
+        nc.vector.tensor_copy(out=y_early[:, high, :], in_=pair_ps[1][:])
+        nc.sync.dma_start(out=out_rows[:, :, early], in_=y_early[:])
+        y_late = values("y_late", PACK, late)
+        for t in range(PACK):
+            acc = bank(t, "y_ps", [P, LATE])
+            second(acc[:], t, zl_w, zl_s)
+            nc.scalar.copy(out=y_late[:, t, :], in_=acc[:])
+        nc.sync.dma_start(out=out_rows[:, :, late], in_=y_late[:])
+
+        planes(y_early, early)
+        planes(y_late, late)
         for q in range(P // QUADRANT):
             queue = nc.sync if q % 2 == 0 else nc.scalar
             queue.dma_start(

@@ -45,11 +45,8 @@ def tile_picked_ymorph_grad_po_kernel(
         nc.gpsimd.memset(xs[:].bitcast(I32), 0)
         nc.sync.dma_start(out=xw[:], in_=x_words[0].rearrange("p n t -> p (n t)").bitcast(I32))
         nc.sync.dma_start(offs_sb[:], offs)
-        for q in range(P // QUADRANT):
-            nc.sync.dma_start(
-                out=xs[QUADRANT * q : QUADRANT * q + PACK, :].bitcast(I32),
-                in_=x_scales[0, PACK * q : PACK * q + PACK, :].bitcast(I32),
-            )
+        for r in range(PACK):
+            nc.sync.dma_start(out=xs[r:P:QUADRANT, :].bitcast(I32), in_=x_scales[0, r : 4 * PACK : PACK, :].bitcast(I32))
 
         w1_rows = w1.rearrange("(p j) c -> p j c", j=PACK)
         w1_pieces = []
@@ -92,7 +89,8 @@ def tile_picked_ymorph_grad_po_kernel(
         w1_bf = keep.tile([P, PACK, P, PACK], BF16, name="w1_bf", align_bytes=64)
         deal(nc.scalar.copy, w1_bf, w1_pieces[0], low)
         deal(nc.scalar.copy, w1_bf, w1_pieces[0], high)
-        deal(nc.vector.tensor_copy, w1_bf, w1_pieces[1])
+        deal(nc.vector.tensor_copy, w1_bf, w1_pieces[1], low)
+        deal(nc.scalar.copy, w1_bf, w1_pieces[1], high)
         deal(nc.vector.tensor_copy, w1_bf, w1_pieces[2], slice(0, 1))
         w1_w = keep.tile([P, H], U32, name="w1_w", tag="w1w", align_bytes=64)
         w1_s = keep.tile([P, H], U8, name="w1_s", align_bytes=64)
@@ -280,9 +278,6 @@ def tile_picked_ymorph_grad_po_kernel(
 
         planes(y_early, early)
         planes(y_late, late)
-        for q in range(P // QUADRANT):
-            queue = nc.sync if q % 2 == 0 else nc.scalar
-            queue.dma_start(
-                out=out_2[0, PACK * q : PACK * q + PACK, :].bitcast(I32),
-                in_=y_s[QUADRANT * q : QUADRANT * q + PACK, :].bitcast(I32),
-            )
+        for r in range(PACK):
+            queue = nc.sync if r % 2 == 0 else nc.scalar
+            queue.dma_start(out=out_2[0, r : 4 * PACK : PACK, :].bitcast(I32), in_=y_s[r:P:QUADRANT, :].bitcast(I32))

@@ -25,7 +25,7 @@ RUN = 4
 
 EARLY = P
 LATE = V - EARLY
-W1_PIECES = [(0, 0, H), (PAIR, 0, H // 2), (PAIR, H // 2, H)]
+W1_PIECES = [(0, 0, H), (PAIR, 0, H)]
 
 
 def tile_picked_ymorph_grad_po_kernel(
@@ -86,12 +86,12 @@ def tile_picked_ymorph_grad_po_kernel(
         nc.vector.tensor_copy(xq_w[:], xw[:].bitcast(U32).indirect(offs_sb[:]))
         nc.vector.tensor_copy(xq_s[:], xs[:].indirect(offs_sb[:]))
 
+        high_rows = w1_pieces[1][1]
         w1_bf = keep.tile([P, PACK, P, PACK], BF16, name="w1_bf", align_bytes=64)
         deal(nc.scalar.copy, w1_bf, w1_pieces[0], low)
         deal(nc.scalar.copy, w1_bf, w1_pieces[0], high)
-        deal(nc.vector.tensor_copy, w1_bf, w1_pieces[1], low)
-        deal(nc.scalar.copy, w1_bf, w1_pieces[1], high)
-        deal(nc.vector.tensor_copy, w1_bf, w1_pieces[2], slice(0, 1))
+        for cols in [slice(0, H // 2), slice(H // 2, H)]:
+            deal(nc.vector.tensor_copy, w1_bf, (w1_pieces[1][0][:, :, cols], high_rows, cols), slice(0, 1))
         w1_w = keep.tile([P, H], U32, name="w1_w", tag="w1w", align_bytes=64)
         w1_s = keep.tile([P, H], U8, name="w1_s", align_bytes=64)
         h = []
@@ -106,8 +106,8 @@ def tile_picked_ymorph_grad_po_kernel(
                 )
             h_t = keep.tile([P, S], F32, name="h%d" % t)
             if t == 0:
-                deal(nc.vector.tensor_copy, w1_bf, w1_pieces[2], slice(1, PAIR))
-                deal(nc.scalar.copy, w1_bf, w1_pieces[2], high)
+                deal(nc.vector.tensor_copy, w1_bf, w1_pieces[1], slice(1, PAIR))
+                deal(nc.scalar.copy, w1_bf, w1_pieces[1], high)
                 shares = [
                     (slice(0, S // 2), nc.scalar.copy),
                     (slice(S // 2, 3 * S // 4), nc.vector.tensor_copy),

@@ -265,16 +265,17 @@ def tile_picked_ymorph_grad_po_kernel(
         for half in halves:
             quantise(zl_w[:, half], zl_s[:, half], z_late[:, half, :])
 
-        y_early = values("y_early", PACK, early, "z_late")
+        y = values("y", PACK, slice(0, V), "z_late")
+        y_early, y_late = y[:, :, early], y[:, :, late]
         nc.scalar.copy(out=y_early[:, low, :], in_=pair_ps[0][:])
         nc.vector.tensor_copy(out=y_early[:, high, :], in_=pair_ps[1][:])
-        nc.sync.dma_start(out=out_rows[:, :, early], in_=y_early[:])
-        y_late = values("y_late", PACK, late)
         for t in range(PACK):
             acc = bank(t, "y_ps", [P, LATE])
             second(acc[:], t, zl_w, zl_s)
             nc.scalar.copy(out=y_late[:, t, :], in_=acc[:])
-        nc.sync.dma_start(out=out_rows[:, :, late], in_=y_late[:])
+            if t % PAIR == PAIR - 1:
+                pair = slice(t + 1 - PAIR, t + 1)
+                nc.sync.dma_start(out=out_rows[:, pair, :], in_=y[:, pair, :])
 
         planes(y_early, early)
         planes(y_late, late)

@@ -22,10 +22,7 @@ PAIR = 2
 QUADRANT = 32
 LIST_COL = 16
 RUN = 4
-
-EARLY = P
-LATE = V - EARLY
-W1_PIECES = [(0, 0, H), (PAIR, 0, H)]
+BLOCKS = H // P
 
 
 def tile_picked_ymorph_grad_po_kernel(
@@ -37,248 +34,238 @@ def tile_picked_ymorph_grad_po_kernel(
         keep = ctx.enter_context(tc.tile_pool(name="keep", bufs=1))
         psum = ctx.enter_context(tc.psum_pool(name="psum", bufs=1))
 
+        def sb(name, shape, dtype, tag=None):
+            return keep.tile(shape, dtype, name=name, tag=tag or name, align_bytes=64)
+
+        def bank(number, name, shape):
+            return psum.tile(shape, F32, name=name, tag="bank%d" % number)
+
         offs_sb = lists.tile([P, S // LIST_COL], U16, name="offs_sb")
         pos_sb = [lists.tile([P, V // LIST_COL], U16, name="pos_sb%d" % i) for i in range(3)]
-
-        xw = keep.tile([P, T], I32, name="xw", align_bytes=64)
-        xs = keep.tile([P, T], U8, name="xs", align_bytes=64)
+        xw = sb("xw", [P, T], I32)
+        xs = sb("xs", [P, T], U8)
         nc.gpsimd.memset(xs[:].bitcast(I32), 0)
         nc.sync.dma_start(out=xw[:], in_=x_words[0].rearrange("p n t -> p (n t)").bitcast(I32))
         nc.sync.dma_start(offs_sb[:], offs)
         for r in range(PACK):
             nc.sync.dma_start(out=xs[r:P:QUADRANT, :].bitcast(I32), in_=x_scales[0, r : 4 * PACK : PACK, :].bitcast(I32))
-
         w1_rows = w1.rearrange("(p j) c -> p j c", j=PACK)
-        w1_pieces = []
-        for j, a, b in W1_PIECES:
-            raw = keep.tile([P, PAIR, b - a], F32, name="w1_raw%d_%d" % (j, a))
-            nc.sync.dma_start(out=raw[:], in_=w1_rows[:, j : j + PAIR, a:b])
-            w1_pieces.append((raw[:], slice(j, j + PAIR), slice(a, b)))
+        w1_raw = []
+        for b in range(BLOCKS):
+            raw = sb("w1_raw%d" % b, [P, PACK, P], F32)
+            nc.sync.dma_start(out=raw[:], in_=w1_rows[:, :, b * P : (b + 1) * P])
+            w1_raw.append(raw)
         for list_sb, pos in zip(pos_sb, [pos1, pos2, pos3]):
             nc.sync.dma_start(list_sb[:], pos)
-        el_sb = keep.tile([P, PACK], F32, name="el_sb")
-        nc.sync.dma_start(out=el_sb[:], in_=el.rearrange("(p t) o -> p (t o)", t=PACK))
+        el_sb = sb("el_sb", [P, BLOCKS], F32)
+        with nc.allow_non_contiguous_dma(reason="one value a partition and block"):
+            nc.sync.dma_start(out=el_sb[:], in_=el.rearrange("(b r) o -> r (b o)", r=P))
         w2_rows = w2.rearrange("(p j) c -> p j c", j=PACK)
-        w2_pieces = []
-        for a in range(0, N, N // 2):
-            raw = keep.tile([P, PACK, N // 2], F32, name="w2_raw%d" % a)
-            nc.sync.dma_start(out=raw[:], in_=w2_rows[:, :, a : a + N // 2])
-            for b in range(0, N // 2, N // 4):
-                w2_pieces.append((raw[:, :, b : b + N // 4], slice(0, PACK), slice(a + b, a + b + N // 4)))
+        w2_raw = []
+        for a in range(2):
+            raw = sb("w2_raw%d" % a, [P, PACK, N // 2], F32)
+            nc.sync.dma_start(out=raw[:], in_=w2_rows[:, :, a * (N // 2) : (a + 1) * (N // 2)])
+            w2_raw.append(raw)
 
-        ident = keep.tile([P, P], F32, name="ident")
+        ident = sb("ident", [P, P], F32)
         make_identity(nc, ident[:])
 
-        def deal(engine_copy, grouped, piece, ts=slice(0, PACK)):
-            raw, js, cols = piece
-            engine_copy(
-                out=grouped[:, ts, cols.start // PACK : cols.stop // PACK, js].rearrange("p t m j -> p m j t"),
-                in_=raw.rearrange("p j (m t) -> p m j t", t=PACK)[:, :, :, ts],
+        def quantise(words, scales, grouped):
+            nc.vector.quantize_mx(out=words.bitcast(FP8X4), scales=scales, in_=grouped)
+
+        def product(acc, l_w, l_s, r_w, r_s):
+            nc.tensor.matmul_mx(
+                out=acc, lhsT=l_w.bitcast(FP8X4), lhsT_scale=l_s, rhs=r_w.bitcast(FP8X4), rhs_scale=r_s,
+                start=True, stop=True,
             )
 
-        def bank(number, name, shape):
-            return psum.tile(shape, F32, name=name, tag="bank%d" % number)
+        w1_w = [sb("w1_w%d" % b, [P, P], U32, tag="xw" if b == 1 else None) for b in range(BLOCKS)]
+        w1_s = [sb("w1_s%d" % b, [P, P], U8) for b in range(BLOCKS)]
+        w1_bf = [sb("w1_bf%d" % b, [P, P, PACK], BF16, tag="xs" if b == 2 else None) for b in range(BLOCKS)]
 
-        low, high = slice(0, PAIR), slice(PAIR, PACK)
+        def round_w1(copy, b):
+            copy(
+                out=w1_bf[b][:].rearrange("p (c i) j -> p c j i", i=RUN),
+                in_=w1_raw[b][:].rearrange("p j (c i) -> p c j i", i=RUN),
+            )
 
-        xq_s = keep.tile([P, S], U8, name="xq_s", align_bytes=64)
-        xq_w = keep.tile([P, S], U32, name="xq_w", align_bytes=64)
-        nc.vector.tensor_copy(xq_w[:], xw[:].bitcast(U32).indirect(offs_sb[:]))
-        nc.vector.tensor_copy(xq_s[:], xs[:].indirect(offs_sb[:]))
+        def quantise_w1(b):
+            quantise(w1_w[b][:], w1_s[b][:], w1_bf[b][:].rearrange("p c j -> p (c j)"))
 
-        high_rows = w1_pieces[1][1]
-        w1_bf = keep.tile([P, PACK, P, PACK], BF16, name="w1_bf", align_bytes=64)
-        deal(nc.scalar.copy, w1_bf, w1_pieces[0], low)
-        deal(nc.scalar.copy, w1_bf, w1_pieces[0], high)
-        for cols in [slice(0, H // 2), slice(H // 2, H)]:
-            deal(nc.vector.tensor_copy, w1_bf, (w1_pieces[1][0][:, :, cols], high_rows, cols), slice(0, 1))
-        w1_w = keep.tile([P, H], U32, name="w1_w", tag="w1w", align_bytes=64)
-        w1_s = keep.tile([P, H], U8, name="w1_s", align_bytes=64)
-        h = []
-        banks_used = 0
-        for t in range(PACK):
-            cols = slice(t * P, (t + 1) * P)
-            for ms in [slice(0, P // 2), slice(P // 2, P)] if t == 0 else [slice(0, P)]:
-                nc.vector.quantize_mx(
-                    out=w1_w[:, cols][:, ms].bitcast(FP8X4),
-                    scales=w1_s[:, cols][:, ms],
-                    in_=w1_bf[:, t, ms].rearrange("p m j -> p (m j)"),
-                )
-            h_t = keep.tile([P, S], F32, name="h%d" % t)
-            if t == 0:
-                deal(nc.vector.tensor_copy, w1_bf, w1_pieces[1], slice(1, PAIR))
-                deal(nc.scalar.copy, w1_bf, w1_pieces[1], high)
-                shares = [
-                    (slice(0, S // 2), nc.scalar.copy),
-                    (slice(S // 2, 3 * S // 4), nc.vector.tensor_copy),
-                    (slice(3 * S // 4, S), nc.scalar.copy),
-                ]
-            else:
-                shares = [(slice(0, S), nc.scalar.copy)]
-            for places, copy_out in shares:
-                acc = bank(banks_used, "h_ps", [P, places.stop - places.start])
-                banks_used = banks_used + 1
-                nc.tensor.matmul_mx(
-                    out=acc[:],
-                    lhsT=w1_w[:, cols].bitcast(FP8X4),
-                    lhsT_scale=w1_s[:, cols],
-                    rhs=xq_w[:, places].bitcast(FP8X4),
-                    rhs_scale=xq_s[:, places],
-                    start=True,
-                    stop=True,
-                )
-                copy_out(out=h_t[:, places], in_=acc[:])
-            h.append(h_t)
+        first_half, second_half = slice(0, S // 2), slice(S // 2, S)
 
-        w2_bf = keep.tile([P, PACK, P, PACK], BF16, name="w2_bf", tag="w1w", align_bytes=64)
-        w2_w = keep.tile([P, N], U32, name="w2_w", align_bytes=64)
-        w2_s = keep.tile([P, N], U8, name="w2_s", align_bytes=64)
+        def picks(places):
+            return offs_sb[:, places.start // LIST_COL : places.stop // LIST_COL]
 
-        y_w = keep.tile([P, V], I32, name="y_w", align_bytes=64)
-        y_s = keep.tile([P, V], U8, name="y_s", align_bytes=64)
-        out_rows = out_0.rearrange("(p t) v -> p t v", t=PACK)
-        out_words = out_1[0].rearrange("p n t -> p (n t)").bitcast(I32)
-        early, late = slice(0, EARLY), slice(EARLY, V)
-        halves = [slice(0, P // 2), slice(P // 2, P)]
+        xq_w = sb("xq_w", [P, S], U32)
+        xq_s = [sb("xq_s0", [P, S // 2], U8), sb("xq_s1", [P, S // 2], U8, tag="w1_raw0")]
+        round_w1(nc.scalar.copy, 0)
+        for places in [first_half, second_half]:
+            nc.vector.tensor_copy(xq_w[:, places], xw[:].bitcast(U32).indirect(picks(places)))
+        nc.vector.tensor_copy(xq_s[0][:], xs[:].indirect(picks(first_half)))
+        quantise_w1(0)
+        nc.vector.tensor_copy(xq_s[1][:], xs[:].indirect(picks(second_half)))
+        round_w1(nc.scalar.copy, 1)
+
+        h = [sb("h%d" % b, [P, S], F32) for b in range(BLOCKS)]
+
+        def layer1(b, places, number):
+            acc = bank(number, "h_ps", [P, places.stop - places.start])
+            for a in range(places.start, places.stop, S // 2):
+                part = slice(a - places.start, a - places.start + S // 2)
+                product(acc[:, part], w1_w[b][:], w1_s[b][:], xq_w[:, a : a + S // 2], xq_s[a // (S // 2)][:])
+            return acc
+
+        acc = layer1(0, first_half, 0)
+        nc.scalar.copy(out=h[0][:, first_half], in_=acc[:])
+        acc = layer1(0, second_half, 1)
+        nc.scalar.copy(out=h[0][:, second_half], in_=acc[:])
+        quantise_w1(1)
+        round_w1(nc.vector.tensor_copy, 2)
+        quantise_w1(2)
+
+        whole = slice(0, V)
+        groups = [slice(0, P), slice(P, V)]
 
         def entries(which, cols):
             return pos_sb[which][:, cols.start // LIST_COL : cols.stop // LIST_COL]
 
-        def values(name, rows, cols, tag=None):
-            return keep.tile([P, rows, cols.stop - cols.start], F32, name=name, tag=tag or name, align_bytes=64)
+        g0 = [sb("g0_%d" % b, [P, V], F32) for b in range(BLOCKS)]
+        d = [sb("d%d" % b, [P, 2, V], F32) for b in range(BLOCKS)]
+        below = [sb("below%d" % b, [P, 2, V], F32) for b in range(BLOCKS)]
+        top = [sb("top%d" % b, [P, V], F32) for b in range(BLOCKS)]
+        zt_bf = [sb("zt_bf%d" % g, [P, PAIR, P, PAIR], BF16) for g in range(2)]
 
-        def rounded(name, cols):
-            return keep.tile([P, cols.stop - cols.start, PACK], BF16, name=name, tag=name, align_bytes=64)
+        def first_scalar(b, cols):
+            nc.scalar.activation(out=g0[b][:, cols], in_=h[b][:].indirect(entries(0, cols)), func=ACT.Copy)
 
-        def first(g0, t, cols):
-            nc.vector.tensor_copy(g0[:, t, :], h[t][:].indirect(entries(0, cols)))
+        def first_vector(b, cols):
+            nc.vector.tensor_copy(g0[b][:, cols], h[b][:].indirect(entries(0, cols)))
 
-        def difference(d, g0, t, which, cols):
-            nc.vector.tensor_tensor(d, h[t][:].indirect(entries(which, cols)), g0[:, t, :], ALU.subtract)
+        def difference(b, i, cols):
+            nc.vector.tensor_tensor(d[b][:, i, cols], h[b][:].indirect(entries(1 + i, cols)), g0[b][:, cols], ALU.subtract)
 
-        def extreme(out, d1, d2, op):
-            nc.vector.scalar_tensor_tensor(out=out, in0=d1, scalar=0.0, in1=d2, op0=op, op1=op)
+        def below_vector(b, i, cols):
+            nc.vector.tensor_scalar(below[b][:, i, cols], d[b][:, i, cols], -1.0, 0.0, ALU.mult, ALU.max)
 
-        def quantise(words, scales, grouped):
-            nc.vector.quantize_mx(out=words.bitcast(FP8X4), scales=scales, in_=grouped.rearrange("p v t -> p (v t)"))
+        def below_scalar(b, rows, cols):
+            nc.scalar.activation(out=below[b][:, rows, cols], in_=d[b][:, rows, cols], func=ACT.Relu, scale=-1.0)
 
-        def second(acc, t, z_w, z_s):
-            cols = slice(t * P, (t + 1) * P)
-            nc.tensor.matmul_mx(
-                out=acc,
-                lhsT=w2_w[:, cols].bitcast(FP8X4),
-                lhsT_scale=w2_s[:, cols],
-                rhs=z_w[:].bitcast(FP8X4),
-                rhs_scale=z_s[:],
-                start=True,
-                stop=True,
-            )
+        def largest(b, cols):
+            nc.vector.tensor_tensor(top[b][:, cols], d[b][:, 0, cols], d[b][:, 1, cols], ALU.max)
 
-        def planes(y, group):
-            parts = [slice(group.start + half.start, group.start + half.stop) for half in halves]
-            y_bfs = [rounded("y_bf%d" % part.start, part) for part in parts]
-            for y_bf, half in zip(y_bfs, halves):
-                nc.vector.tensor_copy(
-                    out=y_bf[:].rearrange("p (c i) t -> p c t i", i=RUN),
-                    in_=y[:, :, half].rearrange("p t (c i) -> p c t i", i=RUN),
-                )
-            for y_bf, part in zip(y_bfs, parts):
-                quantise(y_w[:, part], y_s[:, part], y_bf[:])
-            nc.sync.dma_start(out=out_words[:, group], in_=y_w[:, group])
-
-        g0_early, g0_late = values("g0_early", PACK, early), values("g0_late", PACK, late)
-        d1_last = values("d1_last", 1, late)
-        zt_ps = [bank(5 + u, "zt_ps%d" % u, [P, PAIR, P]) for u in range(2)]
-        zt_bf = [keep.tile([P, P, PAIR], BF16, name="zt_bf%d" % u, tag="zt_bf%d" % u, align_bytes=64) for u in range(2)]
-        zw_ps = bank(7, "zw_ps", [P, 2, P])
-        for t in range(PACK):
-            u, e = divmod(t, PAIR)
-            is_last = t == PACK - 1
-            first(g0_early, t, early)
-            first(g0_late, t, late)
-            d = values("d%d" % t, 3, early)
-            difference(d[:, 0, :], g0_early, t, 1, early)
-            difference(d[:, 1, :], g0_early, t, 2, early)
-            if is_last:
-                difference(d1_last[:, 0, :], g0_late, t, 1, late)
-                nc.vector.tensor_tensor(d[:, 2, :], d[:, 0, :], d[:, 1, :], ALU.subtract)
-            else:
-                nc.gpsimd.tensor_tensor(d[:, 2, :], d[:, 0, :], d[:, 1, :], ALU.subtract)
-            halved = values("halved%d" % t, 3, early)
-            for rows in [slice(0, 2), slice(2, 3)] if is_last else [slice(0, 3)]:
-                nc.scalar.activation(out=halved[:, rows, :], in_=d[:, rows, :], func=ACT.Abs, scale=0.5)
-            if is_last:
-                deal(nc.scalar.copy, w2_bf, w2_pieces[t])
-            terms = [el_sb[:, t : t + 1].to_broadcast([P, P])] + [halved[:, i, :] for i in range(3)]
+        def add_up(acc, b, cols):
+            terms = [el_sb[:, b : b + 1].to_broadcast([P, P]), below[b][:, 0, cols], below[b][:, 1, cols], top[b][:, cols]]
             for i, term in enumerate(terms):
                 nc.tensor.matmul(
-                    out=zt_ps[u][:, e, :],
-                    lhsT=term,
-                    rhs=ident[:],
-                    start=(i == 0),
-                    stop=(i == len(terms) - 1),
-                    is_transpose=True,
+                    out=acc, lhsT=term, rhs=ident[:], start=(i == 0), stop=(i == len(terms) - 1), is_transpose=True
                 )
-            if e == PAIR - 1:
-                nc.scalar.copy(out=zt_bf[u][:], in_=zt_ps[u][:].rearrange("v e p -> v p e"))
-                nc.tensor.transpose(zw_ps[:, u, :], zt_bf[u][:].rearrange("v p e -> v (p e)").bitcast(F32), ident[:])
-            if not is_last:
-                deal(nc.scalar.copy, w2_bf, w2_pieces[t])
-        z_early = rounded("z_early", early)
-        nc.scalar.copy(
-            out=z_early[:].rearrange("p v t -> p (v t)").bitcast(F32).rearrange("p (v u) -> p v u", u=2),
-            in_=zw_ps[:].rearrange("p u v -> p v u"),
-        )
 
-        d_late = values("d_late", 2 * PACK - 1, late, "g0_early")
-        d2_late, d1_most = d_late[:, 0:PACK, :], d_late[:, PACK:, :]
-        most, last = slice(0, PACK - 1), slice(PACK - 1, PACK)
-        hi, up, lo = values("hi", PACK, late), values("up", PACK, late, "zt_bf1"), values("lo", PACK, late)
-        for t in range(PACK - 1):
-            difference(d1_most[:, t, :], g0_late, t, 1, late)
-        for t in range(PACK):
-            difference(d2_late[:, t, :], g0_late, t, 2, late)
-        for ts, d1_ts in [(most, d1_most), (last, d1_last[:])]:
-            extreme(hi[:, ts, :], d1_ts, d2_late[:, ts, :], ALU.max)
-            for t in range(ts.start, ts.stop):
-                nc.scalar.activation(out=up[:, t, :], in_=hi[:, t, :], func=ACT.Identity, bias=el_sb[:, t : t + 1])
-            extreme(lo[:, ts, :], d1_ts, d2_late[:, ts, :], ALU.min)
-
-        quantise(w2_w[:], w2_s[:], w2_bf[:].rearrange("p t m j -> p (t m) j"))
-        ze_w = keep.tile([P, EARLY], U32, name="ze_w", align_bytes=64)
-        ze_s = keep.tile([P, EARLY], U8, name="ze_s", align_bytes=64)
-        quantise(ze_w[:], ze_s[:], z_early[:])
-        pair_ps = [bank(4 + u, "pair_ps%d" % u, [P, PAIR, EARLY]) for u in range(2)]
-        for t in range(PACK):
-            second(pair_ps[t // PAIR][:, t % PAIR, :], t, ze_w, ze_s)
-
-        z_late = rounded("z_late", late)
-        for half in halves:
-            nc.vector.tensor_tensor(
-                z_late[:, half, :].rearrange("p (c i) t -> p c t i", i=RUN),
-                up[:, :, half].rearrange("p t (c i) -> p c t i", i=RUN),
-                lo[:, :, half].rearrange("p t (c i) -> p c t i", i=RUN),
-                ALU.subtract,
+        def round_z(acc, b, g):
+            nc.scalar.copy(
+                out=zt_bf[g][:, :, b * QUADRANT : (b + 1) * QUADRANT, :],
+                in_=acc.rearrange("v (p u e) -> v u p e", u=PAIR, e=PAIR),
             )
-        zl_w = keep.tile([P, LATE], U32, name="zl_w", align_bytes=64)
-        zl_s = keep.tile([P, LATE], U8, name="zl_s", align_bytes=64)
-        for half in halves:
-            quantise(zl_w[:, half], zl_s[:, half], z_late[:, half, :])
 
-        y = values("y", PACK, slice(0, V), "z_late")
-        y_early, y_late = y[:, :, early], y[:, :, late]
-        nc.scalar.copy(out=y_early[:, low, :], in_=pair_ps[0][:])
-        nc.vector.tensor_copy(out=y_early[:, high, :], in_=pair_ps[1][:])
+        def h_out(b):
+            acc = layer1(b, slice(0, S), 1 + b)
+            nc.scalar.copy(out=h[b][:], in_=acc[:])
+
+        first_vector(0, groups[0])
+        first_scalar(0, groups[1])
+        h_out(1)
+        first_scalar(1, whole)
+        round_w1(nc.scalar.copy, 3)
+        quantise_w1(3)
+        sums = []
+        for b in range(BLOCKS - 1):
+            difference(b, 0, whole)
+            difference(b, 1, whole)
+            below_vector(b, 0, whole)
+            largest(b, whole)
+            below_scalar(b, slice(1, 2), whole)
+            acc = bank(5 + b, "zt_ps%d" % b, [P, 2, P])
+            for g in range(2):
+                add_up(acc[:, g, :], b, groups[g])
+            sums.append(acc)
+            if b + 2 < BLOCKS:
+                h_out(b + 2)
+                first_scalar(b + 2, whole)
+            if b >= 1:
+                for g in range(2):
+                    round_z(sums[b - 1][:, g, :], b - 1, g)
+        last = BLOCKS - 1
+        difference(last, 0, groups[0])
+        difference(last, 1, groups[0])
+        difference(last, 0, groups[1])
+        largest(last, groups[0])
+        below_scalar(last, slice(0, 2), groups[0])
+        difference(last, 1, groups[1])
+        below_vector(last, 0, groups[1])
+        largest(last, groups[1])
+        for g in range(2):
+            round_z(sums[last - 1][:, g, :], last - 1, g)
+        below_scalar(last, slice(1, 2), groups[1])
+
+        w2_bf = sb("w2_bf", [P, PACK, P, PACK], BF16, tag="h%d" % last)
+        w2_w = sb("w2_w", [P, N], U32)
+        w2_s = sb("w2_s", [P, N], U8)
+
+        def deal(copy, q):
+            raw = w2_raw[q // 2][:, :, (q % 2) * P : (q % 2 + 1) * P]
+            copy(
+                out=w2_bf[:, :, q * QUADRANT : (q + 1) * QUADRANT, :].rearrange("p t m j -> p m j t"),
+                in_=raw.rearrange("p j (m t) -> p m j t", t=PACK),
+            )
+
+        z_w = [sb("z_w%d" % g, [P, P], U32) for g in range(2)]
+        z_s = [sb("z_s%d" % g, [P, P], U8) for g in range(2)]
+        z = [sb("z%d" % g, [P, P, PACK], BF16) for g in range(2)]
+        for g in range(2):
+            acc = bank(g, "zt_last%d" % g, [P, P])
+            add_up(acc[:], last, groups[g])
+            round_z(acc[:], last, g)
+            turned = bank(2 + g, "turned%d" % g, [P, PAIR, P])
+            for u in range(PAIR):
+                nc.tensor.transpose(turned[:, u, :], zt_bf[g][:, u].rearrange("v p e -> v (p e)").bitcast(F32), ident[:])
+            nc.scalar.copy(
+                out=z[g][:].rearrange("p v t -> p (v t)").bitcast(F32).rearrange("p (v u) -> p v u", u=PAIR),
+                in_=turned[:].rearrange("p u v -> p v u"),
+            )
+        for q in range(PACK):
+            deal(nc.vector.tensor_copy, q)
         for t in range(PACK):
-            acc = bank(t, "y_ps", [P, LATE])
-            second(acc[:], t, zl_w, zl_s)
-            nc.scalar.copy(out=y_late[:, t, :], in_=acc[:])
-            if t % PAIR == PAIR - 1:
-                pair = slice(t + 1 - PAIR, t + 1)
-                nc.sync.dma_start(out=out_rows[:, pair, :], in_=y[:, pair, :])
+            quantise(w2_w[:, t * P : (t + 1) * P], w2_s[:, t * P : (t + 1) * P], w2_bf[:, t].rearrange("p m j -> p (m j)"))
 
-        planes(y_early, early)
-        planes(y_late, late)
+        y_w = sb("y_w", [P, V], I32)
+        y_s = sb("y_s", [P, V], U8)
+        out_rows = out_0.rearrange("(p t) v -> p t v", t=PACK)
+        out_words = out_1[0].rearrange("p n t -> p (n t)").bitcast(I32)
+        ys = []
+        for g in range(2):
+            quantise(z_w[g][:], z_s[g][:], z[g][:].rearrange("p v t -> p (v t)"))
+            y = sb("y%d" % g, [P, PACK, P], F32)
+            for u in range(PAIR):
+                acc = bank(4 + 2 * g + u, "y_ps", [P, PAIR, P])
+                for e in range(PAIR):
+                    cols = slice((PAIR * u + e) * P, (PAIR * u + e + 1) * P)
+                    product(acc[:, e, :], w2_w[:, cols], w2_s[:, cols], z_w[g][:], z_s[g][:])
+                copy = nc.scalar.copy if u == 0 else nc.vector.tensor_copy
+                copy(out=y[:, PAIR * u : PAIR * (u + 1), :], in_=acc[:])
+            nc.sync.dma_start(out=out_rows[:, :, groups[g]], in_=y[:])
+            ys.append(y)
+        halves = [slice(0, P // 2), slice(P // 2, P)]
+        for g in range(2):
+            y_bf = sb("y_bf%d" % g, [P, P, PACK], BF16)
+            for half in halves:
+                nc.vector.tensor_copy(
+                    out=y_bf[:, half, :].rearrange("p (c i) t -> p c t i", i=RUN),
+                    in_=ys[g][:, :, half].rearrange("p t (c i) -> p c t i", i=RUN),
+                )
+            for half in halves:
+                part = slice(groups[g].start + half.start, groups[g].start + half.stop)
+                quantise(y_w[:, part], y_s[:, part], y_bf[:, half, :].rearrange("p v t -> p (v t)"))
+            nc.sync.dma_start(out=out_words[:, groups[g]], in_=y_w[:, groups[g]])
         for r in range(PACK):
             queue = nc.sync if r % 2 == 0 else nc.scalar
             queue.dma_start(out=out_2[0, r : 4 * PACK : PACK, :].bitcast(I32), in_=y_s[r:P:QUADRANT, :].bitcast(I32))

@@ -55,17 +55,21 @@ def tile_picked_ymorph_grad_po_kernel(
             raw = sb("w1_raw%d" % b, [P, PACK, P], F32)
             nc.sync.dma_start(out=raw[:], in_=w1_rows[:, :, b * P : (b + 1) * P])
             w1_raw.append(raw)
-        for list_sb, pos in zip(pos_sb, [pos1, pos2, pos3]):
-            nc.sync.dma_start(list_sb[:], pos)
+            if b == 2:
+                for list_sb, pos in zip(pos_sb, [pos1, pos2, pos3]):
+                    nc.sync.dma_start(list_sb[:], pos)
         el_sb = sb("el_sb", [P, BLOCKS], F32)
         with nc.allow_non_contiguous_dma(reason="one value a partition and block"):
             nc.sync.dma_start(out=el_sb[:], in_=el.rearrange("(b r) o -> r (b o)", r=P))
         w2_rows = w2.rearrange("(p j) c -> p j c", j=PACK)
         w2_raw = []
-        for a in range(2):
-            raw = sb("w2_raw%d" % a, [P, PACK, N // 2], F32)
+
+        def load_w2(a, tag):
+            raw = sb("w2_raw%d" % a, [P, PACK, N // 2], F32, tag=tag)
             nc.sync.dma_start(out=raw[:], in_=w2_rows[:, :, a * (N // 2) : (a + 1) * (N // 2)])
             w2_raw.append(raw)
+
+        load_w2(0, None)
 
         ident = sb("ident", [P, P], F32)
         make_identity(nc, ident[:])
@@ -81,7 +85,7 @@ def tile_picked_ymorph_grad_po_kernel(
 
         w1_w = [sb("w1_w%d" % b, [P, P], U32, tag="xw" if b == 1 else None) for b in range(BLOCKS)]
         w1_s = [sb("w1_s%d" % b, [P, P], U8) for b in range(BLOCKS)]
-        w1_bf = [sb("w1_bf%d" % b, [P, P, PACK], BF16, tag="xs" if b == 2 else None) for b in range(BLOCKS)]
+        w1_bf = [sb("w1_bf%d" % b, [P, P, PACK], BF16, tag="xs" if b == 3 else None) for b in range(BLOCKS)]
 
         def round_w1(copy, b):
             copy(
@@ -106,6 +110,7 @@ def tile_picked_ymorph_grad_po_kernel(
         quantise_w1(0)
         nc.vector.tensor_copy(xq_s[1][:], xs[:].indirect(picks(second_half)))
         round_w1(nc.scalar.copy, 1)
+        round_w1(nc.scalar.copy, 2)
 
         h = [sb("h%d" % b, [P, S], F32) for b in range(BLOCKS)]
 
@@ -121,8 +126,9 @@ def tile_picked_ymorph_grad_po_kernel(
         acc = layer1(0, second_half, 1)
         nc.scalar.copy(out=h[0][:, second_half], in_=acc[:])
         quantise_w1(1)
-        round_w1(nc.vector.tensor_copy, 2)
+        round_w1(nc.vector.tensor_copy, 3)
         quantise_w1(2)
+        quantise_w1(3)
 
         whole = slice(0, V)
         groups = [slice(0, P), slice(P, V)]
@@ -134,7 +140,7 @@ def tile_picked_ymorph_grad_po_kernel(
         d = [sb("d%d" % b, [P, 2, V], F32) for b in range(BLOCKS)]
         below = [sb("below%d" % b, [P, 2, V], F32) for b in range(BLOCKS)]
         top = [sb("top%d" % b, [P, V], F32) for b in range(BLOCKS)]
-        zt_bf = [sb("zt_bf%d" % g, [P, PAIR, P, PAIR], BF16) for g in range(2)]
+        zt_bf = sb("zt_bf", [P, 2, PAIR, P, PAIR], BF16)
 
         def first_scalar(b, cols):
             nc.scalar.activation(out=g0[b][:, cols], in_=h[b][:].indirect(entries(0, cols)), func=ACT.Copy)
@@ -161,10 +167,19 @@ def tile_picked_ymorph_grad_po_kernel(
                     out=acc, lhsT=term, rhs=ident[:], start=(i == 0), stop=(i == len(terms) - 1), is_transpose=True
                 )
 
-        def round_z(acc, b, g):
+        def round_z(acc, b, gs):
             nc.scalar.copy(
-                out=zt_bf[g][:, :, b * QUADRANT : (b + 1) * QUADRANT, :],
-                in_=acc.rearrange("v (p u e) -> v u p e", u=PAIR, e=PAIR),
+                out=zt_bf[:, gs, :, b * QUADRANT : (b + 1) * QUADRANT, :],
+                in_=acc.rearrange("v g (p u e) -> v g u p e", u=PAIR, e=PAIR),
+            )
+
+        w2_bf = sb("w2_bf", [P, PACK, P, PACK], BF16, tag="g0_1")
+
+        def deal(copy, q):
+            raw = w2_raw[q // 2][:, :, (q % 2) * P : (q % 2 + 1) * P]
+            copy(
+                out=w2_bf[:, :, q * QUADRANT : (q + 1) * QUADRANT, :].rearrange("p t m j -> p m j t"),
+                in_=raw.rearrange("p j (m t) -> p m j t", t=PACK),
             )
 
         def h_out(b):
@@ -175,25 +190,29 @@ def tile_picked_ymorph_grad_po_kernel(
         first_scalar(0, groups[1])
         h_out(1)
         first_scalar(1, whole)
-        round_w1(nc.scalar.copy, 3)
-        quantise_w1(3)
         sums = []
         for b in range(BLOCKS - 1):
             difference(b, 0, whole)
             difference(b, 1, whole)
             below_vector(b, 0, whole)
             largest(b, whole)
+            if b == 1:
+                load_w2(1, "h1")
+                h_out(3)
+            if b == 2:
+                round_z(sums[0][:], 0, slice(0, 2))
+                deal(nc.scalar.copy, 0)
             below_scalar(b, slice(1, 2), whole)
-            acc = bank(5 + b, "zt_ps%d" % b, [P, 2, P])
+            acc = bank(2 + b, "zt_ps%d" % b, [P, 2, P])
             for g in range(2):
                 add_up(acc[:, g, :], b, groups[g])
             sums.append(acc)
+            if b == 0:
+                h_out(2)
             if b + 2 < BLOCKS:
-                h_out(b + 2)
                 first_scalar(b + 2, whole)
-            if b >= 1:
-                for g in range(2):
-                    round_z(sums[b - 1][:, g, :], b - 1, g)
+        round_z(sums[1][:], 1, slice(0, 2))
+        deal(nc.scalar.copy, 1)
         last = BLOCKS - 1
         difference(last, 0, groups[0])
         difference(last, 1, groups[0])
@@ -203,39 +222,30 @@ def tile_picked_ymorph_grad_po_kernel(
         difference(last, 1, groups[1])
         below_vector(last, 0, groups[1])
         largest(last, groups[1])
-        for g in range(2):
-            round_z(sums[last - 1][:, g, :], last - 1, g)
+        round_z(sums[last - 1][:], last - 1, slice(0, 2))
         below_scalar(last, slice(1, 2), groups[1])
 
-        w2_bf = sb("w2_bf", [P, PACK, P, PACK], BF16, tag="h%d" % last)
         w2_w = sb("w2_w", [P, N], U32)
         w2_s = sb("w2_s", [P, N], U8)
-
-        def deal(copy, q):
-            raw = w2_raw[q // 2][:, :, (q % 2) * P : (q % 2 + 1) * P]
-            copy(
-                out=w2_bf[:, :, q * QUADRANT : (q + 1) * QUADRANT, :].rearrange("p t m j -> p m j t"),
-                in_=raw.rearrange("p j (m t) -> p m j t", t=PACK),
-            )
-
         z_w = [sb("z_w%d" % g, [P, P], U32) for g in range(2)]
         z_s = [sb("z_s%d" % g, [P, P], U8) for g in range(2)]
         z = [sb("z%d" % g, [P, P, PACK], BF16) for g in range(2)]
         for g in range(2):
-            acc = bank(g, "zt_last%d" % g, [P, P])
-            add_up(acc[:], last, groups[g])
-            round_z(acc[:], last, g)
-            turned = bank(2 + g, "turned%d" % g, [P, PAIR, P])
+            acc = bank(2 + g, "zt_last%d" % g, [P, 1, P])
+            add_up(acc[:, 0, :], last, groups[g])
+            round_z(acc[:], last, slice(g, g + 1))
+            turned = bank(g, "turned%d" % g, [P, PAIR, P])
             for u in range(PAIR):
-                nc.tensor.transpose(turned[:, u, :], zt_bf[g][:, u].rearrange("v p e -> v (p e)").bitcast(F32), ident[:])
+                nc.tensor.transpose(turned[:, u, :], zt_bf[:, g, u].rearrange("v p e -> v (p e)").bitcast(F32), ident[:])
             nc.scalar.copy(
                 out=z[g][:].rearrange("p v t -> p (v t)").bitcast(F32).rearrange("p (v u) -> p v u", u=PAIR),
                 in_=turned[:].rearrange("p u v -> p v u"),
             )
-        for q in range(PACK):
+        for q in range(2, PACK):
             deal(nc.vector.tensor_copy, q)
-        for t in range(PACK):
-            quantise(w2_w[:, t * P : (t + 1) * P], w2_s[:, t * P : (t + 1) * P], w2_bf[:, t].rearrange("p m j -> p (m j)"))
+        for u in range(PAIR):
+            cols = slice(u * N // 2, (u + 1) * N // 2)
+            quantise(w2_w[:, cols], w2_s[:, cols], w2_bf[:, PAIR * u : PAIR * (u + 1)].rearrange("p t m j -> p (t m j)"))
 
         y_w = sb("y_w", [P, V], I32)
         y_s = sb("y_s", [P, V], U8)

@@ -51,16 +51,14 @@ def tile_picked_ymorph_grad_po_kernel(
             nc.sync.dma_start(out=xs[r:P:QUADRANT, :].bitcast(I32), in_=x_scales[0, r : 4 * PACK : PACK, :].bitcast(I32))
         w1_rows = w1.rearrange("(p j) c -> p j c", j=PACK)
         w1_raw = []
-        for b in range(BLOCKS):
-            raw = sb("w1_raw%d" % b, [P, PACK, P], F32)
-            nc.sync.dma_start(out=raw[:], in_=w1_rows[:, :, b * P : (b + 1) * P])
-            w1_raw.append(raw)
-            if b == 2:
-                for list_sb, pos in zip(pos_sb, [pos1, pos2, pos3]):
-                    nc.sync.dma_start(list_sb[:], pos)
-        el_sb = sb("el_sb", [P, BLOCKS], F32)
-        with nc.allow_non_contiguous_dma(reason="one value a partition and block"):
-            nc.sync.dma_start(out=el_sb[:], in_=el.rearrange("(b r) o -> r (b o)", r=P))
+        for a in range(2):
+            raw = sb("w1_raw%d" % a, [P, PACK, H // 2], F32)
+            nc.sync.dma_start(out=raw[:], in_=w1_rows[:, :, a * (H // 2) : (a + 1) * (H // 2)])
+            w1_raw.append(raw[:].rearrange("p j (m t) -> p m j t", t=PACK))
+        for list_sb, pos in zip(pos_sb, [pos1, pos2, pos3]):
+            nc.sync.dma_start(list_sb[:], pos)
+        el_sb = sb("el_sb", [P, PACK], F32)
+        nc.sync.dma_start(out=el_sb[:], in_=el.rearrange("(p t) o -> p (t o)", t=PACK))
         w2_rows = w2.rearrange("(p j) c -> p j c", j=PACK)
         w2_raw = []
 
@@ -70,6 +68,7 @@ def tile_picked_ymorph_grad_po_kernel(
             w2_raw.append(raw)
 
         load_w2(0, None)
+        load_w2(1, None)
 
         ident = sb("ident", [P, P], F32)
         make_identity(nc, ident[:])
@@ -83,18 +82,24 @@ def tile_picked_ymorph_grad_po_kernel(
                 start=True, stop=True,
             )
 
-        w1_w = [sb("w1_w%d" % b, [P, P], U32, tag="xw" if b == 1 else None) for b in range(BLOCKS)]
-        w1_s = [sb("w1_s%d" % b, [P, P], U8) for b in range(BLOCKS)]
-        w1_bf = [sb("w1_bf%d" % b, [P, P, PACK], BF16, tag="xs" if b == 3 else None) for b in range(BLOCKS)]
+        HALF = P // 2
+        low, high = slice(0, PAIR), slice(PAIR, PACK)
+        w1_w = sb("w1_w", [P, H], U32)
+        w1_s = sb("w1_s", [P, H], U8)
+        low_bf = [sb("low_bf%d" % a, [P, PAIR, HALF, PACK], BF16) for a in range(2)]
+        high_bf = sb("high_bf", [P, PAIR, P, PACK], BF16, tag="low_bf0")
 
-        def round_w1(copy, b):
+        def round_low(copy, a):
+            copy(out=low_bf[a][:].rearrange("p t m j -> p m j t"), in_=w1_raw[a][:, :, :, low])
+
+        def round_high(copy, a):
             copy(
-                out=w1_bf[b][:].rearrange("p (c i) j -> p c j i", i=RUN),
-                in_=w1_raw[b][:].rearrange("p j (c i) -> p c j i", i=RUN),
+                out=high_bf[:, :, a * HALF : (a + 1) * HALF, :].rearrange("p t m j -> p m j t"),
+                in_=w1_raw[a][:, :, :, high],
             )
 
-        def quantise_w1(b):
-            quantise(w1_w[b][:], w1_s[b][:], w1_bf[b][:].rearrange("p c j -> p (c j)"))
+        def quantise_w1(cols, grouped):
+            quantise(w1_w[:, cols], w1_s[:, cols], grouped[:].rearrange("p t m j -> p (t m j)"))
 
         first_half, second_half = slice(0, S // 2), slice(S // 2, S)
 
@@ -102,45 +107,42 @@ def tile_picked_ymorph_grad_po_kernel(
             return offs_sb[:, places.start // LIST_COL : places.stop // LIST_COL]
 
         xq_w = sb("xq_w", [P, S], U32)
-        xq_s = [sb("xq_s0", [P, S // 2], U8), sb("xq_s1", [P, S // 2], U8, tag="w1_raw0")]
-        round_w1(nc.scalar.copy, 0)
-        for places in [first_half, second_half]:
-            nc.vector.tensor_copy(xq_w[:, places], xw[:].bitcast(U32).indirect(picks(places)))
-        nc.vector.tensor_copy(xq_s[0][:], xs[:].indirect(picks(first_half)))
-        quantise_w1(0)
-        nc.vector.tensor_copy(xq_s[1][:], xs[:].indirect(picks(second_half)))
-        round_w1(nc.scalar.copy, 1)
-        round_w1(nc.scalar.copy, 2)
+        xq_s = sb("xq_s", [P, S], U8)
+        round_low(nc.scalar.copy, 0)
+        nc.vector.tensor_copy(xq_w[:], xw[:].bitcast(U32).indirect(offs_sb[:]))
+        nc.vector.tensor_copy(xq_s[:], xs[:].indirect(offs_sb[:]))
+        quantise_w1(slice(0, P), low_bf[0])
+        round_low(nc.scalar.copy, 1)
 
         h = [sb("h%d" % b, [P, S], F32) for b in range(BLOCKS)]
 
         def layer1(b, places, number):
             acc = bank(number, "h_ps", [P, places.stop - places.start])
-            for a in range(places.start, places.stop, S // 2):
-                part = slice(a - places.start, a - places.start + S // 2)
-                product(acc[:, part], w1_w[b][:], w1_s[b][:], xq_w[:, a : a + S // 2], xq_s[a // (S // 2)][:])
-            return acc
+            cols = slice(b * P, (b + 1) * P)
+            product(acc[:], w1_w[:, cols], w1_s[:, cols], xq_w[:, places], xq_s[:, places])
+            nc.scalar.copy(out=h[b][:, places], in_=acc[:])
 
-        acc = layer1(0, first_half, 0)
-        nc.scalar.copy(out=h[0][:, first_half], in_=acc[:])
-        acc = layer1(0, second_half, 1)
-        nc.scalar.copy(out=h[0][:, second_half], in_=acc[:])
-        quantise_w1(1)
-        round_w1(nc.vector.tensor_copy, 3)
-        quantise_w1(2)
-        quantise_w1(3)
+        layer1(0, first_half, 0)
+        layer1(0, second_half, 1)
+        round_high(nc.vector.tensor_copy, 0)
+        round_high(nc.vector.tensor_copy, 1)
+        quantise_w1(slice(P, 2 * P), low_bf[1])
+        quantise_w1(slice(2 * P, H), high_bf)
 
         whole = slice(0, V)
         groups = [slice(0, P), slice(P, V)]
+        last = BLOCKS - 1
 
         def entries(which, cols):
             return pos_sb[which][:, cols.start // LIST_COL : cols.stop // LIST_COL]
 
         g0 = [sb("g0_%d" % b, [P, V], F32) for b in range(BLOCKS)]
         d = [sb("d%d" % b, [P, 2, V], F32) for b in range(BLOCKS)]
-        below = [sb("below%d" % b, [P, 2, V], F32) for b in range(BLOCKS)]
-        top = [sb("top%d" % b, [P, V], F32) for b in range(BLOCKS)]
-        zt_bf = sb("zt_bf", [P, 2, PAIR, P, PAIR], BF16)
+        below = [sb("below%d" % b, [P, 2, V], F32) for b in range(PAIR)]
+        top = [sb("top%d" % b, [P, V], F32) for b in range(PAIR)]
+        zt_bf = sb("zt_bf", [P, 2, P, PAIR], BF16)
+        pairs = sb("pairs", [P, PAIR, V, PAIR], BF16)
+        pair_words = pairs[:].rearrange("p u v e -> p u (v e)").bitcast(F32)
 
         def first_scalar(b, cols):
             nc.scalar.activation(out=g0[b][:, cols], in_=h[b][:].indirect(entries(0, cols)), func=ACT.Copy)
@@ -151,101 +153,89 @@ def tile_picked_ymorph_grad_po_kernel(
         def difference(b, i, cols):
             nc.vector.tensor_tensor(d[b][:, i, cols], h[b][:].indirect(entries(1 + i, cols)), g0[b][:, cols], ALU.subtract)
 
-        def below_vector(b, i, cols):
-            nc.vector.tensor_scalar(below[b][:, i, cols], d[b][:, i, cols], -1.0, 0.0, ALU.mult, ALU.max)
+        def add_term(acc, term, start=False, stop=False):
+            nc.tensor.matmul(out=acc, lhsT=term, rhs=ident[:], start=start, stop=stop, is_transpose=True)
 
-        def below_scalar(b, rows, cols):
-            nc.scalar.activation(out=below[b][:, rows, cols], in_=d[b][:, rows, cols], func=ACT.Relu, scale=-1.0)
-
-        def largest(b, cols):
-            nc.vector.tensor_tensor(top[b][:, cols], d[b][:, 0, cols], d[b][:, 1, cols], ALU.max)
-
-        def add_up(acc, b, cols):
-            terms = [el_sb[:, b : b + 1].to_broadcast([P, P]), below[b][:, 0, cols], below[b][:, 1, cols], top[b][:, cols]]
-            for i, term in enumerate(terms):
-                nc.tensor.matmul(
-                    out=acc, lhsT=term, rhs=ident[:], start=(i == 0), stop=(i == len(terms) - 1), is_transpose=True
-                )
-
-        def round_z(acc, b, gs):
-            nc.scalar.copy(
-                out=zt_bf[:, gs, :, b * QUADRANT : (b + 1) * QUADRANT, :],
-                in_=acc.rearrange("v g (p u e) -> v g u p e", u=PAIR, e=PAIR),
-            )
+        first_vector(0, groups[0])
+        first_scalar(0, groups[1])
+        layer1(1, slice(0, S), 2)
+        first_scalar(1, whole)
+        low_ps = bank(0, "low_ps", [P, 2, PAIR, P])
+        for g in range(2):
+            for e in range(PAIR):
+                add_term(low_ps[:, g, e, :], el_sb[:, e : e + 1].to_broadcast([P, P]), start=(g == 0 and e == 0))
+        for b in range(PAIR):
+            difference(b, 0, whole)
+            difference(b, 1, whole)
+            nc.vector.tensor_scalar(below[b][:, 0, :], d[b][:, 0, :], -1.0, 0.0, ALU.mult, ALU.max)
+            nc.vector.tensor_tensor(top[b][:], d[b][:, 0, :], d[b][:, 1, :], ALU.max)
+            layer1(b + 2, slice(0, S), 3 + b)
+            first_scalar(b + 2, whole)
+            if b == 1:
+                g2 = sb("g2", [P, V], F32)
+                nc.scalar.activation(out=g2[:], in_=h[last][:].indirect(entries(2, whole)), func=ACT.Copy)
+            nc.scalar.activation(out=below[b][:, 1, :], in_=d[b][:, 1, :], func=ACT.Relu, scale=-1.0)
+            for g in range(2):
+                for i, term in enumerate([below[b][:, 0, :], below[b][:, 1, :], top[b][:]]):
+                    add_term(
+                        low_ps[:, g, :, b * HALF : (b + 1) * HALF], term[:, groups[g]], stop=(b == 1 and g == 1 and i == 2)
+                    )
 
         w2_bf = sb("w2_bf", [P, PACK, P, PACK], BF16, tag="g0_1")
 
-        def deal(copy, q):
+        def deal(q):
             raw = w2_raw[q // 2][:, :, (q % 2) * P : (q % 2 + 1) * P]
-            copy(
+            nc.scalar.copy(
                 out=w2_bf[:, :, q * QUADRANT : (q + 1) * QUADRANT, :].rearrange("p t m j -> p m j t"),
                 in_=raw.rearrange("p j (m t) -> p m j t", t=PACK),
             )
 
-        def h_out(b):
-            acc = layer1(b, slice(0, S), 1 + b)
-            nc.scalar.copy(out=h[b][:], in_=acc[:])
+        deal(0)
+        nc.scalar.copy(out=zt_bf[:], in_=low_ps[:].rearrange("v g e p -> v g p e"))
+        turned = bank(1, "turned", [P, 2, P])
+        for g in range(2):
+            nc.tensor.transpose(turned[:, g, :], zt_bf[:, g].rearrange("v p e -> v (p e)").bitcast(F32), ident[:])
+        deal(1)
+        nc.scalar.copy(out=pair_words[:, 0, :], in_=turned[:].rearrange("p g v -> p (g v)"))
+        deal(2)
+        deal(3)
 
-        first_vector(0, groups[0])
-        first_scalar(0, groups[1])
-        h_out(1)
-        first_scalar(1, whole)
-        sums = []
-        for b in range(BLOCKS - 1):
-            difference(b, 0, whole)
-            difference(b, 1, whole)
-            below_vector(b, 0, whole)
-            largest(b, whole)
-            if b == 1:
-                load_w2(1, "h1")
-                h_out(3)
-            if b == 2:
-                round_z(sums[0][:], 0, slice(0, 2))
-                deal(nc.scalar.copy, 0)
-            below_scalar(b, slice(1, 2), whole)
-            acc = bank(2 + b, "zt_ps%d" % b, [P, 2, P])
-            for g in range(2):
-                add_up(acc[:, g, :], b, groups[g])
-            sums.append(acc)
-            if b == 0:
-                h_out(2)
-            if b + 2 < BLOCKS:
-                first_scalar(b + 2, whole)
-        round_z(sums[1][:], 1, slice(0, 2))
-        deal(nc.scalar.copy, 1)
-        last = BLOCKS - 1
-        difference(last, 0, groups[0])
-        difference(last, 1, groups[0])
-        difference(last, 0, groups[1])
-        largest(last, groups[0])
-        below_scalar(last, slice(0, 2), groups[0])
-        difference(last, 1, groups[1])
-        below_vector(last, 0, groups[1])
-        largest(last, groups[1])
-        round_z(sums[last - 1][:], last - 1, slice(0, 2))
-        below_scalar(last, slice(1, 2), groups[1])
+        ends = [sb("ends2", [P, 2, V], F32, tag="d1"), sb("ends3", [P, 2, V], F32)]
 
-        w2_w = sb("w2_w", [P, N], U32)
+        def extremes(b, cols):
+            for i, op in enumerate([ALU.max, ALU.min]):
+                nc.vector.scalar_tensor_tensor(
+                    out=ends[b - PAIR][:, i, cols], in0=d[b][:, 0, cols], scalar=0.0, in1=d[b][:, 1, cols], op0=op, op1=op
+                )
+
+        def spread(b, cols):
+            nc.vector.scalar_tensor_tensor(
+                out=pairs[:, 1, cols, b - PAIR], in0=ends[b - PAIR][:, 0, cols], scalar=el_sb[:, b : b + 1],
+                in1=ends[b - PAIR][:, 1, cols], op0=ALU.add, op1=ALU.subtract,
+            )
+
+        w2_w = sb("w2_w", [P, N], U32, tag="g0_3")
         w2_s = sb("w2_s", [P, N], U8)
-        z_w = [sb("z_w%d" % g, [P, P], U32) for g in range(2)]
-        z_s = [sb("z_s%d" % g, [P, P], U8) for g in range(2)]
+        difference(2, 0, whole)
+        difference(2, 1, whole)
+        difference(last, 0, whole)
+        nc.vector.tensor_tensor(d[last][:, 1, :], g2[:], g0[last][:], ALU.subtract)
+        extremes(2, whole)
+        extremes(last, whole)
+        spread(2, whole)
+        for cols in groups:
+            spread(last, cols)
         z = [sb("z%d" % g, [P, P, PACK], BF16) for g in range(2)]
         for g in range(2):
-            acc = bank(2 + g, "zt_last%d" % g, [P, 1, P])
-            add_up(acc[:, 0, :], last, groups[g])
-            round_z(acc[:], last, slice(g, g + 1))
-            turned = bank(g, "turned%d" % g, [P, PAIR, P])
-            for u in range(PAIR):
-                nc.tensor.transpose(turned[:, u, :], zt_bf[:, g, u].rearrange("v p e -> v (p e)").bitcast(F32), ident[:])
             nc.scalar.copy(
                 out=z[g][:].rearrange("p v t -> p (v t)").bitcast(F32).rearrange("p (v u) -> p v u", u=PAIR),
-                in_=turned[:].rearrange("p u v -> p v u"),
+                in_=pair_words[:, :, groups[g]].rearrange("p u v -> p v u"),
             )
-        for q in range(2, PACK):
-            deal(nc.vector.tensor_copy, q)
         for u in range(PAIR):
             cols = slice(u * N // 2, (u + 1) * N // 2)
             quantise(w2_w[:, cols], w2_s[:, cols], w2_bf[:, PAIR * u : PAIR * (u + 1)].rearrange("p t m j -> p (t m j)"))
+        z_w = [sb("z_w%d" % g, [P, P], U32) for g in range(2)]
+        z_s = [sb("z_s%d" % g, [P, P], U8) for g in range(2)]
 
         y_w = sb("y_w", [P, V], I32)
         y_s = sb("y_s", [P, V], U8)
@@ -260,7 +250,7 @@ def tile_picked_ymorph_grad_po_kernel(
                 for e in range(PAIR):
                     cols = slice((PAIR * u + e) * P, (PAIR * u + e + 1) * P)
                     product(acc[:, e, :], w2_w[:, cols], w2_s[:, cols], z_w[g][:], z_s[g][:])
-                copy = nc.scalar.copy if u == 0 else nc.vector.tensor_copy
+                copy = nc.vector.tensor_copy if u == 1 else nc.scalar.copy
                 copy(out=y[:, PAIR * u : PAIR * (u + 1), :], in_=acc[:])
             nc.sync.dma_start(out=out_rows[:, :, groups[g]], in_=y[:])
             ys.append(y)

@@ -86,8 +86,8 @@ def tile_picked_ymorph_grad_po_kernel(
         low, high = slice(0, PAIR), slice(PAIR, PACK)
         w1_w = sb("w1_w", [P, H], U32)
         w1_s = sb("w1_s", [P, H], U8)
-        low_bf = [sb("low_bf%d" % a, [P, PAIR, HALF, PACK], BF16) for a in range(2)]
-        high_bf = sb("high_bf", [P, PAIR, P, PACK], BF16, tag="low_bf0")
+        low_bf = [sb("low_bf%d" % a, [P, PAIR, HALF, PACK], BF16, tag="low_bf") for a in range(2)]
+        high_bf = sb("high_bf", [P, PAIR, P, PACK], BF16)
 
         def round_low(copy, a):
             copy(out=low_bf[a][:].rearrange("p t m j -> p m j t"), in_=w1_raw[a][:, :, :, low])
@@ -112,7 +112,8 @@ def tile_picked_ymorph_grad_po_kernel(
         nc.vector.tensor_copy(xq_w[:], xw[:].bitcast(U32).indirect(offs_sb[:]))
         nc.vector.tensor_copy(xq_s[:], xs[:].indirect(offs_sb[:]))
         quantise_w1(slice(0, P), low_bf[0])
-        round_low(nc.scalar.copy, 1)
+        round_high(nc.scalar.copy, 0)
+        round_high(nc.scalar.copy, 1)
 
         h = [sb("h%d" % b, [P, S], F32) for b in range(BLOCKS)]
 
@@ -124,8 +125,7 @@ def tile_picked_ymorph_grad_po_kernel(
 
         layer1(0, first_half, 0)
         layer1(0, second_half, 1)
-        round_high(nc.vector.tensor_copy, 0)
-        round_high(nc.vector.tensor_copy, 1)
+        round_low(nc.vector.tensor_copy, 1)
         quantise_w1(slice(P, 2 * P), low_bf[1])
         quantise_w1(slice(2 * P, H), high_bf)
 
@@ -181,61 +181,62 @@ def tile_picked_ymorph_grad_po_kernel(
                         low_ps[:, g, :, b * HALF : (b + 1) * HALF], term[:, groups[g]], stop=(b == 1 and g == 1 and i == 2)
                     )
 
-        w2_bf = sb("w2_bf", [P, PACK, P, PACK], BF16, tag="g0_1")
+        w2_bf = [sb("w2_bf%d" % u, [P, PAIR, P, PACK], BF16, tag=tag) for u, tag in enumerate(["g0_1", "top1"])]
 
-        def deal(q):
-            raw = w2_raw[q // 2][:, :, (q % 2) * P : (q % 2 + 1) * P]
+        def deal(u, a):
             nc.scalar.copy(
-                out=w2_bf[:, :, q * QUADRANT : (q + 1) * QUADRANT, :].rearrange("p t m j -> p m j t"),
-                in_=raw.rearrange("p j (m t) -> p m j t", t=PACK),
+                out=w2_bf[u][:, :, a * HALF : (a + 1) * HALF, :].rearrange("p t m j -> p m j t"),
+                in_=w2_raw[a][:].rearrange("p j (m t) -> p m j t", t=PACK)[:, :, :, PAIR * u : PAIR * (u + 1)],
             )
 
-        deal(0)
+        deal(0, 0)
+        deal(0, 1)
         nc.scalar.copy(out=zt_bf[:], in_=low_ps[:].rearrange("v g e p -> v g p e"))
         turned = bank(1, "turned", [P, 2, P])
         for g in range(2):
             nc.tensor.transpose(turned[:, g, :], zt_bf[:, g].rearrange("v p e -> v (p e)").bitcast(F32), ident[:])
-        deal(1)
+        deal(1, 0)
         nc.scalar.copy(out=pair_words[:, 0, :], in_=turned[:].rearrange("p g v -> p (g v)"))
-        deal(2)
-        deal(3)
+        deal(1, 1)
 
-        ends = [sb("ends2", [P, 2, V], F32, tag="d1"), sb("ends3", [P, 2, V], F32)]
-
-        def extremes(b, cols):
+        def extremes(b, cols, tag=None):
+            ends = sb("ends%d_%d" % (b, cols.start), [P, 2, cols.stop - cols.start], F32, tag=tag)
             for i, op in enumerate([ALU.max, ALU.min]):
                 nc.vector.scalar_tensor_tensor(
-                    out=ends[b - PAIR][:, i, cols], in0=d[b][:, 0, cols], scalar=0.0, in1=d[b][:, 1, cols], op0=op, op1=op
+                    out=ends[:, i, :], in0=d[b][:, 0, cols], scalar=0.0, in1=d[b][:, 1, cols], op0=op, op1=op
                 )
+            return ends
 
-        def spread(b, cols):
+        def spread(b, cols, ends):
             nc.vector.scalar_tensor_tensor(
-                out=pairs[:, 1, cols, b - PAIR], in0=ends[b - PAIR][:, 0, cols], scalar=el_sb[:, b : b + 1],
-                in1=ends[b - PAIR][:, 1, cols], op0=ALU.add, op1=ALU.subtract,
+                out=pairs[:, 1, cols, b - PAIR], in0=ends[:, 0, :], scalar=el_sb[:, b : b + 1],
+                in1=ends[:, 1, :], op0=ALU.add, op1=ALU.subtract,
             )
 
-        w2_w = sb("w2_w", [P, N], U32, tag="g0_3")
         w2_s = sb("w2_s", [P, N], U8)
         difference(2, 0, whole)
         difference(2, 1, whole)
         difference(last, 0, whole)
         nc.vector.tensor_tensor(d[last][:, 1, :], g2[:], g0[last][:], ALU.subtract)
-        extremes(2, whole)
-        extremes(last, whole)
-        spread(2, whole)
-        for cols in groups:
-            spread(last, cols)
+        ends = extremes(2, whole, "d1")
+        last_ends = [extremes(last, groups[0])]
+        spread(2, whole, ends)
+        last_ends.append(extremes(last, groups[1]))
+        for cols, ends in zip(groups, last_ends):
+            spread(last, cols, ends)
+        w2_w = sb("w2_w", [P, N], U32, tag="ends3_0")
         z = [sb("z%d" % g, [P, P, PACK], BF16) for g in range(2)]
         for g in range(2):
             nc.scalar.copy(
                 out=z[g][:].rearrange("p v t -> p (v t)").bitcast(F32).rearrange("p (v u) -> p v u", u=PAIR),
                 in_=pair_words[:, :, groups[g]].rearrange("p u v -> p v u"),
             )
-        for u in range(PAIR):
-            cols = slice(u * N // 2, (u + 1) * N // 2)
-            quantise(w2_w[:, cols], w2_s[:, cols], w2_bf[:, PAIR * u : PAIR * (u + 1)].rearrange("p t m j -> p (t m j)"))
         z_w = [sb("z_w%d" % g, [P, P], U32) for g in range(2)]
         z_s = [sb("z_s%d" % g, [P, P], U8) for g in range(2)]
+        for u in range(PAIR):
+            cols = slice(u * N // 2, (u + 1) * N // 2)
+            quantise(w2_w[:, cols], w2_s[:, cols], w2_bf[u][:].rearrange("p t m j -> p (t m j)"))
+            quantise(z_w[u][:], z_s[u][:], z[u][:].rearrange("p v t -> p (v t)"))
 
         y_w = sb("y_w", [P, V], I32)
         y_s = sb("y_s", [P, V], U8)
@@ -243,7 +244,6 @@ def tile_picked_ymorph_grad_po_kernel(
         out_words = out_1[0].rearrange("p n t -> p (n t)").bitcast(I32)
         ys = []
         for g in range(2):
-            quantise(z_w[g][:], z_s[g][:], z[g][:].rearrange("p v t -> p (v t)"))
             y = sb("y%d" % g, [P, PACK, P], F32)
             for u in range(PAIR):
                 acc = bank(4 + 2 * g + u, "y_ps", [P, PAIR, P])

@@ -156,9 +156,9 @@ def tile_picked_ymorph_grad_po_kernel(
         def add_term(acc, term, start=False, stop=False):
             nc.tensor.matmul(out=acc, lhsT=term, rhs=ident[:], start=start, stop=stop, is_transpose=True)
 
-        first_vector(0, groups[0])
-        first_scalar(0, groups[1])
-        layer1(1, slice(0, S), 2)
+        first_vector(0, whole)
+        layer1(1, first_half, 2)
+        layer1(1, second_half, 5)
         first_scalar(1, whole)
         low_ps = bank(0, "low_ps", [P, 2, PAIR, P])
         for g in range(2):
@@ -169,12 +169,13 @@ def tile_picked_ymorph_grad_po_kernel(
             difference(b, 1, whole)
             nc.vector.tensor_scalar(below[b][:, 0, :], d[b][:, 0, :], -1.0, 0.0, ALU.mult, ALU.max)
             nc.vector.tensor_tensor(top[b][:], d[b][:, 0, :], d[b][:, 1, :], ALU.max)
+            nc.vector.tensor_scalar(below[b][:, 1, :], d[b][:, 1, :], -1.0, 0.0, ALU.mult, ALU.max)
             layer1(b + 2, slice(0, S), 3 + b)
             first_scalar(b + 2, whole)
             if b == 1:
-                g2 = sb("g2", [P, V], F32)
-                nc.scalar.activation(out=g2[:], in_=h[last][:].indirect(entries(2, whole)), func=ACT.Copy)
-            nc.scalar.activation(out=below[b][:, 1, :], in_=d[b][:, 1, :], func=ACT.Relu, scale=-1.0)
+                g12 = sb("g12", [P, 2, V], F32)
+                for i in range(2):
+                    nc.scalar.activation(out=g12[:, i, :], in_=h[last][:].indirect(entries(1 + i, whole)), func=ACT.Copy)
             for g in range(2):
                 for i, term in enumerate([below[b][:, 0, :], below[b][:, 1, :], top[b][:]]):
                     add_term(
@@ -216,8 +217,7 @@ def tile_picked_ymorph_grad_po_kernel(
         w2_s = sb("w2_s", [P, N], U8)
         difference(2, 0, whole)
         difference(2, 1, whole)
-        difference(last, 0, whole)
-        nc.vector.tensor_tensor(d[last][:, 1, :], g2[:], g0[last][:], ALU.subtract)
+        nc.vector.tensor_tensor(d[last][:], g12[:], g0[last][:].unsqueeze(1).to_broadcast([P, 2, V]), ALU.subtract)
         ends = extremes(2, whole, "d1")
         last_ends = [extremes(last, groups[0])]
         spread(2, whole, ends)
@@ -250,12 +250,11 @@ def tile_picked_ymorph_grad_po_kernel(
                 for e in range(PAIR):
                     cols = slice((PAIR * u + e) * P, (PAIR * u + e + 1) * P)
                     product(acc[:, e, :], w2_w[:, cols], w2_s[:, cols], z_w[g][:], z_s[g][:])
-                copy = nc.vector.tensor_copy if u == 1 else nc.scalar.copy
+                copy = nc.vector.tensor_copy if (g, u) == (0, 1) else nc.scalar.copy
                 copy(out=y[:, PAIR * u : PAIR * (u + 1), :], in_=acc[:])
             nc.sync.dma_start(out=out_rows[:, :, groups[g]], in_=y[:])
             ys.append(y)
-        halves = [slice(0, P // 2), slice(P // 2, P)]
-        for g in range(2):
+        for g, halves in enumerate([[slice(0, P)], [slice(0, P // 2), slice(P // 2, P)]]):
             y_bf = sb("y_bf%d" % g, [P, P, PACK], BF16)
             for half in halves:
                 nc.vector.tensor_copy(

@@ -184,14 +184,13 @@ def tile_picked_ymorph_grad_po_kernel(
 
         w2_bf = [sb("w2_bf%d" % u, [P, PAIR, P, PACK], BF16, tag=tag) for u, tag in enumerate(["g0_1", "top1"])]
 
-        def deal(u, a):
-            nc.scalar.copy(
+        def deal(u, a, copy=nc.scalar.copy):
+            copy(
                 out=w2_bf[u][:, :, a * HALF : (a + 1) * HALF, :].rearrange("p t m j -> p m j t"),
                 in_=w2_raw[a][:].rearrange("p j (m t) -> p m j t", t=PACK)[:, :, :, PAIR * u : PAIR * (u + 1)],
             )
 
         deal(0, 0)
-        deal(0, 1)
         nc.scalar.copy(out=zt_bf[:], in_=low_ps[:].rearrange("v g e p -> v g p e"))
         turned = bank(1, "turned", [P, 2, P])
         for g in range(2):
@@ -218,6 +217,7 @@ def tile_picked_ymorph_grad_po_kernel(
         difference(2, 0, whole)
         difference(2, 1, whole)
         nc.vector.tensor_tensor(d[last][:], g12[:], g0[last][:].unsqueeze(1).to_broadcast([P, 2, V]), ALU.subtract)
+        deal(0, 1, nc.vector.tensor_copy)
         ends = extremes(2, whole, "d1")
         last_ends = [extremes(last, groups[0])]
         spread(2, whole, ends)

@@ -156,7 +156,8 @@ def tile_picked_ymorph_grad_po_kernel(
         def add_term(acc, term, start=False, stop=False):
             nc.tensor.matmul(out=acc, lhsT=term, rhs=ident[:], start=start, stop=stop, is_transpose=True)
 
-        first_vector(0, whole)
+        for cols in groups:
+            first_vector(0, cols)
         layer1(1, first_half, 2)
         layer1(1, second_half, 5)
         first_scalar(1, whole)
@@ -165,7 +166,8 @@ def tile_picked_ymorph_grad_po_kernel(
             for e in range(PAIR):
                 add_term(low_ps[:, g, e, :], el_sb[:, e : e + 1].to_broadcast([P, P]), start=(g == 0 and e == 0))
         for b in range(PAIR):
-            difference(b, 0, whole)
+            for cols in groups if b == 0 else [whole]:
+                difference(b, 0, cols)
             difference(b, 1, whole)
             nc.vector.tensor_scalar(below[b][:, 0, :], d[b][:, 0, :], -1.0, 0.0, ALU.mult, ALU.max)
             nc.vector.tensor_tensor(top[b][:], d[b][:, 0, :], d[b][:, 1, :], ALU.max)
@@ -242,29 +244,31 @@ def tile_picked_ymorph_grad_po_kernel(
         y_s = sb("y_s", [P, V], U8)
         out_rows = out_0.rearrange("(p t) v -> p t v", t=PACK)
         out_words = out_1[0].rearrange("p n t -> p (n t)").bitcast(I32)
-        ys = []
+        y = sb("y", [P, PACK, V], F32)
+        ys = [y[:, :, cols] for cols in groups]
         for g in range(2):
-            y = sb("y%d" % g, [P, PACK, P], F32)
             for u in range(PAIR):
                 acc = bank(4 + 2 * g + u, "y_ps", [P, PAIR, P])
                 for e in range(PAIR):
                     cols = slice((PAIR * u + e) * P, (PAIR * u + e + 1) * P)
                     product(acc[:, e, :], w2_w[:, cols], w2_s[:, cols], z_w[g][:], z_s[g][:])
                 copy = nc.vector.tensor_copy if (g, u) == (0, 1) else nc.scalar.copy
-                copy(out=y[:, PAIR * u : PAIR * (u + 1), :], in_=acc[:])
-            nc.sync.dma_start(out=out_rows[:, :, groups[g]], in_=y[:])
-            ys.append(y)
-        for g, halves in enumerate([[slice(0, P)], [slice(0, P // 2), slice(P // 2, P)]]):
-            y_bf = sb("y_bf%d" % g, [P, P, PACK], BF16)
-            for half in halves:
-                nc.vector.tensor_copy(
-                    out=y_bf[:, half, :].rearrange("p (c i) t -> p c t i", i=RUN),
-                    in_=ys[g][:, :, half].rearrange("p t (c i) -> p c t i", i=RUN),
-                )
-            for half in halves:
-                part = slice(groups[g].start + half.start, groups[g].start + half.stop)
-                quantise(y_w[:, part], y_s[:, part], y_bf[:, half, :].rearrange("p v t -> p (v t)"))
-            nc.sync.dma_start(out=out_words[:, groups[g]], in_=y_w[:, groups[g]])
+                rows = slice(PAIR * u, PAIR * (u + 1))
+                copy(out=ys[g][:, rows, :], in_=acc[:])
+                if g == 1:
+                    nc.sync.dma_start(out=out_rows[:, rows, groups[g]], in_=ys[g][:, rows, :])
+            if g == 0:
+                nc.sync.dma_start(out=out_rows[:, :, groups[g]], in_=ys[g])
+        y_bf = sb("y_bf", [P, V, PACK], BF16)
+        quarter = V // 4
+        for part in [slice(0, P), slice(P, P + quarter), slice(P + quarter, V)]:
+            nc.vector.tensor_copy(
+                out=y_bf[:, part, :].rearrange("p (c i) t -> p c t i", i=RUN),
+                in_=y[:, :, part].rearrange("p t (c i) -> p c t i", i=RUN),
+            )
+        for part in [slice(0, quarter), slice(quarter, 3 * quarter), slice(3 * quarter, V)]:
+            quantise(y_w[:, part], y_s[:, part], y_bf[:, part, :].rearrange("p v t -> p (v t)"))
+        nc.sync.dma_start(out=out_words, in_=y_w[:])
         for r in range(PACK):
             queue = nc.sync if r % 2 == 0 else nc.scalar
             queue.dma_start(out=out_2[0, r : 4 * PACK : PACK, :].bitcast(I32), in_=y_s[r:P:QUADRANT, :].bitcast(I32))

@@ -178,8 +178,8 @@ def tile_picked_ymorph_grad_po_kernel(
                 g12 = sb("g12", [P, 2, V], F32)
                 for i in range(2):
                     nc.scalar.activation(out=g12[:, i, :], in_=h[last][:].indirect(entries(1 + i, whole)), func=ACT.Copy)
-            for g in range(2):
-                for i, term in enumerate([below[b][:, 0, :], below[b][:, 1, :], top[b][:]]):
+            for i, term in enumerate([below[b][:, 0, :], top[b][:], below[b][:, 1, :]]):
+                for g in range(2):
                     add_term(
                         low_ps[:, g, :, b * HALF : (b + 1) * HALF], term[:, groups[g]], stop=(b == 1 and g == 1 and i == 2)
                     )
@@ -193,9 +193,9 @@ def tile_picked_ymorph_grad_po_kernel(
             )
 
         deal(0, 0)
-        nc.scalar.copy(out=zt_bf[:], in_=low_ps[:].rearrange("v g e p -> v g p e"))
         turned = bank(1, "turned", [P, 2, P])
         for g in range(2):
+            nc.scalar.copy(out=zt_bf[:, g], in_=low_ps[:, g].rearrange("v e p -> v p e"))
             nc.tensor.transpose(turned[:, g, :], zt_bf[:, g].rearrange("v p e -> v (p e)").bitcast(F32), ident[:])
         deal(1, 0)
         nc.scalar.copy(out=pair_words[:, 0, :], in_=turned[:].rearrange("p g v -> p (g v)"))

from contextlib import ExitStack

import concourse.mybir as mybir
from concourse.masks import make_identity

K, T, S, V, H, N = 512, 1024, 512, 256, 512, 512
FLOPS = 2 * K * H * S + 2 * H * N * V

F32 = mybir.dt.float32
BF16 = mybir.dt.bfloat16
I32 = mybir.dt.int32
U32 = mybir.dt.uint32
U16 = mybir.dt.uint16
U8 = mybir.dt.uint8
FP8X4 = mybir.dt.float8_e4m3fn_x4
ALU = mybir.AluOpType
ACT = mybir.ActivationFunctionType

P = 128
PACK = 4
PAIR = 2
QUADRANT = 32
LIST_COL = 16
RUN = 4
BLOCKS = H // P


def tile_picked_ymorph_grad_po_kernel(
    tc, x_words, x_scales, w1, w2, el, offs, pos1, pos2, pos3, out_0, out_1, out_2
):
    nc = tc.nc
    with ExitStack() as ctx:
        lists = ctx.enter_context(tc.tile_pool(name="lists", bufs=1))
        keep = ctx.enter_context(tc.tile_pool(name="keep", bufs=1))
        psum = ctx.enter_context(tc.psum_pool(name="psum", bufs=1))

        def sb(name, shape, dtype, tag=None):
            return keep.tile(shape, dtype, name=name, tag=tag or name, align_bytes=64)

        def bank(number, name, shape):
            return psum.tile(shape, F32, name=name, tag="bank%d" % number)

        offs_sb = lists.tile([P, S // LIST_COL], U16, name="offs_sb")
        pos_sb = [lists.tile([P, V // LIST_COL], U16, name="pos_sb%d" % i) for i in range(3)]
        xw = sb("xw", [P, T], I32)
        xs = sb("xs", [P, T], U8)
        nc.gpsimd.memset(xs[:].bitcast(I32), 0)
        nc.sync.dma_start(out=xw[:], in_=x_words[0].rearrange("p n t -> p (n t)").bitcast(I32))
        nc.sync.dma_start(offs_sb[:], offs)
        for r in range(PACK):
            nc.sync.dma_start(out=xs[r:P:QUADRANT, :].bitcast(I32), in_=x_scales[0, r : 4 * PACK : PACK, :].bitcast(I32))
        w1_rows = w1.rearrange("(p j) c -> p j c", j=PACK)
        w1_raw = []
        for a in range(2):
            raw = sb("w1_raw%d" % a, [P, PACK, H // 2], F32)
            nc.sync.dma_start(out=raw[:], in_=w1_rows[:, :, a * (H // 2) : (a + 1) * (H // 2)])
            w1_raw.append(raw[:].rearrange("p j (m t) -> p m j t", t=PACK))
        for list_sb, pos in zip(pos_sb, [pos1, pos2, pos3]):
            nc.sync.dma_start(list_sb[:], pos)
        el_sb = sb("el_sb", [P, PACK], F32)
        nc.sync.dma_start(out=el_sb[:], in_=el.rearrange("(p t) o -> p (t o)", t=PACK))
        w2_rows = w2.rearrange("(p j) c -> p j c", j=PACK)
        w2_raw = []

        def load_w2(a, tag):
            raw = sb("w2_raw%d" % a, [P, PACK, N // 2], F32, tag=tag)
            nc.sync.dma_start(out=raw[:], in_=w2_rows[:, :, a * (N // 2) : (a + 1) * (N // 2)])
            w2_raw.append(raw)

        load_w2(0, None)
        load_w2(1, None)

        ident = sb("ident", [P, P], F32)
        make_identity(nc, ident[:])

        def quantise(words, scales, grouped):
            nc.vector.quantize_mx(out=words.bitcast(FP8X4), scales=scales, in_=grouped)

        def product(acc, l_w, l_s, r_w, r_s):
            nc.tensor.matmul_mx(
                out=acc, lhsT=l_w.bitcast(FP8X4), lhsT_scale=l_s, rhs=r_w.bitcast(FP8X4), rhs_scale=r_s,
                start=True, stop=True,
            )

        HALF = P // 2
        low, high = slice(0, PAIR), slice(PAIR, PACK)
        w1_w = sb("w1_w", [P, H], U32)
        w1_s = sb("w1_s", [P, H], U8)
        low_bf = [sb("low_bf%d" % a, [P, PAIR, HALF, PACK], BF16, tag="low_bf") for a in range(2)]
        high_bf = sb("high_bf", [P, PAIR, P, PACK], BF16)

        def round_low(copy, a):
            copy(out=low_bf[a][:].rearrange("p t m j -> p m j t"), in_=w1_raw[a][:, :, :, low])

        def round_high(copy, a):
            copy(
                out=high_bf[:, :, a * HALF : (a + 1) * HALF, :].rearrange("p t m j -> p m j t"),
                in_=w1_raw[a][:, :, :, high],
            )

        def quantise_w1(cols, grouped):
            quantise(w1_w[:, cols], w1_s[:, cols], grouped[:].rearrange("p t m j -> p (t m j)"))

        first_half, second_half = slice(0, S // 2), slice(S // 2, S)

        def picks(places):
            return offs_sb[:, places.start // LIST_COL : places.stop // LIST_COL]

        xq_w = sb("xq_w", [P, S], U32)
        xq_s = sb("xq_s", [P, S], U8)
        round_low(nc.scalar.copy, 0)
        nc.vector.tensor_copy(xq_w[:], xw[:].bitcast(U32).indirect(offs_sb[:]))
        nc.vector.tensor_copy(xq_s[:], xs[:].indirect(offs_sb[:]))
        quantise_w1(slice(0, P), low_bf[0])
        round_high(nc.scalar.copy, 0)
        round_high(nc.scalar.copy, 1)

        h = [sb("h%d" % b, [P, S], F32) for b in range(BLOCKS)]

        def layer1(b, places, number):
            acc = bank(number, "h_ps", [P, places.stop - places.start])
            cols = slice(b * P, (b + 1) * P)
            product(acc[:], w1_w[:, cols], w1_s[:, cols], xq_w[:, places], xq_s[:, places])
            nc.scalar.copy(out=h[b][:, places], in_=acc[:])

        layer1(0, first_half, 0)
        layer1(0, second_half, 1)
        round_low(nc.vector.tensor_copy, 1)
        quantise_w1(slice(P, 2 * P), low_bf[1])
        quantise_w1(slice(2 * P, H), high_bf)

        whole = slice(0, V)
        groups = [slice(0, P), slice(P, V)]
        last = BLOCKS - 1

        def entries(which, cols):
            return pos_sb[which][:, cols.start // LIST_COL : cols.stop // LIST_COL]

        g0 = [sb("g0_%d" % b, [P, V], F32) for b in range(BLOCKS)]
        d = [sb("d%d" % b, [P, 2, V], F32) for b in range(BLOCKS)]
        below = [sb("below%d" % b, [P, 2, V], F32) for b in range(PAIR)]
        top = [sb("top%d" % b, [P, V], F32) for b in range(PAIR)]
        zt_bf = sb("zt_bf", [P, 2, P, PAIR], BF16)
        pairs = sb("pairs", [P, PAIR, V, PAIR], BF16)
        pair_words = pairs[:].rearrange("p u v e -> p u (v e)").bitcast(F32)

        def first_scalar(b, cols):
            nc.scalar.activation(out=g0[b][:, cols], in_=h[b][:].indirect(entries(0, cols)), func=ACT.Copy)

        def first_vector(b, cols):
            nc.vector.tensor_copy(g0[b][:, cols], h[b][:].indirect(entries(0, cols)))

        def difference(b, i, cols):
            nc.vector.tensor_tensor(d[b][:, i, cols], h[b][:].indirect(entries(1 + i, cols)), g0[b][:, cols], ALU.subtract)

        def add_term(acc, term, start=False, stop=False):
            nc.tensor.matmul(out=acc, lhsT=term, rhs=ident[:], start=start, stop=stop, is_transpose=True)

        for cols in groups:
            first_vector(0, cols)
        layer1(1, first_half, 2)
        layer1(1, second_half, 5)
        first_scalar(1, whole)
        low_ps = bank(0, "low_ps", [P, 2, PAIR, P])
        for g in range(2):
            for e in range(PAIR):
                add_term(low_ps[:, g, e, :], el_sb[:, e : e + 1].to_broadcast([P, P]), start=(g == 0 and e == 0))
        for b in range(PAIR):
            for cols in groups if b == 0 else [whole]:
                difference(b, 0, cols)
            difference(b, 1, whole)
            nc.vector.tensor_scalar(below[b][:, 0, :], d[b][:, 0, :], -1.0, 0.0, ALU.mult, ALU.max)
            nc.vector.tensor_tensor(top[b][:], d[b][:, 0, :], d[b][:, 1, :], ALU.max)
            nc.vector.tensor_scalar(below[b][:, 1, :], d[b][:, 1, :], -1.0, 0.0, ALU.mult, ALU.max)
            layer1(b + 2, slice(0, S), 3 + b)
            first_scalar(b + 2, whole)
            if b == 1:
                g12 = sb("g12", [P, 2, V], F32)
                for i in range(2):
                    nc.scalar.activation(out=g12[:, i, :], in_=h[last][:].indirect(entries(1 + i, whole)), func=ACT.Copy)
            for i, term in enumerate([below[b][:, 0, :], top[b][:], below[b][:, 1, :]]):
                for g in range(2):
                    add_term(
                        low_ps[:, g, :, b * HALF : (b + 1) * HALF], term[:, groups[g]], stop=(b == 1 and g == 1 and i == 2)
                    )

        w2_bf = [sb("w2_bf%d" % u, [P, PAIR, P, PACK], BF16, tag=tag) for u, tag in enumerate(["g0_1", "top1"])]

        def deal(u, a, copy=nc.scalar.copy):
            copy(
                out=w2_bf[u][:, :, a * HALF : (a + 1) * HALF, :].rearrange("p t m j -> p m j t"),
                in_=w2_raw[a][:].rearrange("p j (m t) -> p m j t", t=PACK)[:, :, :, PAIR * u : PAIR * (u + 1)],
            )

        deal(0, 0)
        turned = bank(1, "turned", [P, 2, P])
        for g in range(2):
            nc.scalar.copy(out=zt_bf[:, g], in_=low_ps[:, g].rearrange("v e p -> v p e"))
            nc.tensor.transpose(turned[:, g, :], zt_bf[:, g].rearrange("v p e -> v (p e)").bitcast(F32), ident[:])
        deal(1, 0)
        nc.scalar.copy(out=pair_words[:, 0, :], in_=turned[:].rearrange("p g v -> p (g v)"))
        deal(1, 1)

        def extremes(b, cols, tag=None):
            ends = sb("ends%d_%d" % (b, cols.start), [P, 2, cols.stop - cols.start], F32, tag=tag)
            for i, op in enumerate([ALU.max, ALU.min]):
                nc.vector.scalar_tensor_tensor(
                    out=ends[:, i, :], in0=d[b][:, 0, cols], scalar=0.0, in1=d[b][:, 1, cols], op0=op, op1=op
                )
            return ends

        def spread(b, cols, ends):
            nc.vector.scalar_tensor_tensor(
                out=pairs[:, 1, cols, b - PAIR], in0=ends[:, 0, :], scalar=el_sb[:, b : b + 1],
                in1=ends[:, 1, :], op0=ALU.add, op1=ALU.subtract,
            )

        w2_s = sb("w2_s", [P, N], U8)
        difference(2, 0, whole)
        difference(2, 1, whole)
        nc.vector.tensor_tensor(d[last][:], g12[:], g0[last][:].unsqueeze(1).to_broadcast([P, 2, V]), ALU.subtract)
        deal(0, 1, nc.vector.tensor_copy)
        ends = extremes(2, whole, "d1")
        last_ends = [extremes(last, groups[0])]
        spread(2, whole, ends)
        last_ends.append(extremes(last, groups[1]))
        for cols, ends in zip(groups, last_ends):
            spread(last, cols, ends)
        w2_w = sb("w2_w", [P, N], U32, tag="ends3_0")
        z = [sb("z%d" % g, [P, P, PACK], BF16) for g in range(2)]
        for g in range(2):
            nc.scalar.copy(
                out=z[g][:].rearrange("p v t -> p (v t)").bitcast(F32).rearrange("p (v u) -> p v u", u=PAIR),
                in_=pair_words[:, :, groups[g]].rearrange("p u v -> p v u"),
            )
        z_w = [sb("z_w%d" % g, [P, P], U32) for g in range(2)]
        z_s = [sb("z_s%d" % g, [P, P], U8) for g in range(2)]
        for u in range(PAIR):
            cols = slice(u * N // 2, (u + 1) * N // 2)
            quantise(w2_w[:, cols], w2_s[:, cols], w2_bf[u][:].rearrange("p t m j -> p (t m j)"))
            quantise(z_w[u][:], z_s[u][:], z[u][:].rearrange("p v t -> p (v t)"))

        y_w = sb("y_w", [P, V], I32)
        y_s = sb("y_s", [P, V], U8)
        out_rows = out_0.rearrange("(p t) v -> p t v", t=PACK)
        out_words = out_1[0].rearrange("p n t -> p (n t)").bitcast(I32)
        y = sb("y", [P, PACK, V], F32)
        ys = [y[:, :, cols] for cols in groups]
        for g in range(2):
            for u in range(PAIR):
                acc = bank(4 + 2 * g + u, "y_ps", [P, PAIR, P])
                for e in range(PAIR):
                    cols = slice((PAIR * u + e) * P, (PAIR * u + e + 1) * P)
                    product(acc[:, e, :], w2_w[:, cols], w2_s[:, cols], z_w[g][:], z_s[g][:])
                copy = nc.vector.tensor_copy if (g, u) == (0, 1) else nc.scalar.copy
                rows = slice(PAIR * u, PAIR * (u + 1))
                copy(out=ys[g][:, rows, :], in_=acc[:])
                if g == 1:
                    nc.sync.dma_start(out=out_rows[:, rows, groups[g]], in_=ys[g][:, rows, :])
            if g == 0:
                nc.sync.dma_start(out=out_rows[:, :, groups[g]], in_=ys[g])
        y_bf = sb("y_bf", [P, V, PACK], BF16)
        quarter = V // 4
        for part in [slice(0, P), slice(P, P + quarter), slice(P + quarter, V)]:
            nc.vector.tensor_copy(
                out=y_bf[:, part, :].rearrange("p (c i) t -> p c t i", i=RUN),
                in_=y[:, :, part].rearrange("p t (c i) -> p c t i", i=RUN),
            )
        for part in [slice(0, quarter), slice(quarter, 3 * quarter), slice(3 * quarter, V)]:
            quantise(y_w[:, part], y_s[:, part], y_bf[:, part, :].rearrange("p v t -> p (v t)"))
        nc.sync.dma_start(out=out_words, in_=y_w[:])
        for r in range(PACK):
            queue = nc.sync if r % 2 == 0 else nc.scalar
            queue.dma_start(out=out_2[0, r : 4 * PACK : PACK, :].bitcast(I32), in_=y_s[r:P:QUADRANT, :].bitcast(I32))
